import numpy as np
import ml_dtypes


def mxq(x, axis, fmt="e4m3"):
    dtype, down = {"e4m3": (ml_dtypes.float8_e4m3fn, 7), "e5m2": (ml_dtypes.float8_e5m2, 14)}[fmt]
    v = np.moveaxis(np.asarray(x, np.float32).astype(ml_dtypes.bfloat16).astype(np.float64), axis, -1)
    blocks = v.reshape(v.shape[:-1] + (-1, 32))
    amax = np.abs(blocks).max(-1, keepdims=True)
    byte = np.maximum(np.where(amax > 0, np.frexp(amax)[1] - 1 + 127, 0) - down, 1)
    scale = np.exp2(byte - 127.0)
    codes = (blocks / scale).astype(np.float32).astype(dtype).astype(np.float64)
    return np.moveaxis((codes * scale).reshape(v.shape), -1, axis)


WIDE = False


def mx_kscale(k):
    if not WIDE:
        return np.ones(k)
    levels = np.array([10, -10, 5, -5, 0])
    if k % 512:
        return np.exp2(np.random.permutation(np.resize(levels, k // 32))).repeat(32)
    a = np.empty((k // 512, 16))
    for p in range(k // 512):
        a[p, :8] = np.random.permutation(np.resize(levels, 8))
        for g in range(8):
            far = levels[np.abs(levels - a[p, g]) >= 10]
            a[p, g + 8] = far[np.random.randint(len(far))]
    return np.exp2(a.ravel()).repeat(32)


def f64(x):
    return np.asarray(x).astype(np.float64)


def striped8(idx):
    return np.concatenate([v.reshape(-1, 16).T for v in idx]).astype(np.uint16)


def unstriped8(offs):
    return np.stack([offs[16 * g:16 * g + 16].T.reshape(-1) for g in range(8)]).astype(np.int64)


E2M1 = np.array([0.0, 0.5, 1.0, 1.5, 2.0, 3.0, 4.0, 6.0, -0.0, -0.5, -1.0, -1.5, -2.0, -3.0, -4.0, -6.0])


def pack_weight(w, fmt):
    k, n = w.shape
    w = f64(np.asarray(w, np.float32).astype(ml_dtypes.bfloat16)).reshape(k // 32, 32, n)
    amax = np.abs(w).max(1)
    if fmt == "e4m3":
        byte = np.frexp(amax)[1] - 1 + 127 - 7
    else:
        mant, ex = np.frexp(amax / 6.0)
        byte = np.where(mant > 0.5, ex, ex - 1) + 127
    byte = np.clip(np.where(amax > 0, byte, 1), 1, 254)
    scaled = (w * np.exp2(127.0 - byte)[:, None, :]).reshape(k, n).astype(np.float32)
    by_word = np.ascontiguousarray(scaled.reshape(k // 512, 128, 4, n).transpose(0, 1, 3, 2))
    if fmt == "e4m3":
        words = by_word.astype(ml_dtypes.float8_e4m3fn).view(np.uint8)
    else:
        c = by_word.astype(ml_dtypes.float4_e2m1fn).view(np.uint8) & 0xF
        words = (c[..., 0::2] | (c[..., 1::2] << 4)).reshape(k // 512, 128, 2 * n)
    return np.ascontiguousarray(words), np.ascontiguousarray(byte.astype(np.uint8).reshape(k // 512, 16, n))


def unpack_weight(words, scales, fmt):
    g, _, n = scales.shape
    words = np.ascontiguousarray(words).reshape(g, 128, n, -1)
    if fmt == "e4m3":
        vals = words.view(ml_dtypes.float8_e4m3fn).astype(np.float64)
    else:
        nib = np.empty((g, 128, n, 4), np.uint8)
        nib[..., 0::2] = words & 0xF
        nib[..., 1::2] = words >> 4
        vals = E2M1[nib]
    vals = vals * np.repeat(np.exp2(scales.astype(np.float64) - 127.0), 8, axis=1)[..., None]
    return vals.transpose(0, 1, 3, 2).reshape(g * 512, n)


K, H, M, T, S = 1024, 512, 128, 1024, 512


def setup_inputs():
    n = np.random.standard_normal
    s = mx_kscale(K)[:, None]
    u = mx_kscale(H)[:, None]
    p_w2 = pack_weight(1.4 * n((H, M)) / np.sqrt(H) / u, "e2m1")
    return {
        "xT": (n((K, T)) * s).astype(np.float32),
        "w1": (n((K, H)) / np.sqrt(K) / s * u.T).astype(np.float32),
        "w2_words": p_w2[0],
        "w2_scales": p_w2[1],
        "wgt": np.repeat(np.random.uniform(0.5, 2.0, (8, S)), 16, axis=0).astype(np.float32),
        "b": (0.3 * n(128)).astype(np.float32),
        "offs": striped8(np.stack([np.random.permutation(T)[:S] for _ in range(8)])),
    }


def reference(xT, w1, w2_words, w2_scales, wgt, b, offs):
    idx = unstriped8(offs)
    group = np.arange(K) % 512 // 64
    xg = f64(wgt)[np.arange(K) // 4 % 128] * f64(xT)[np.arange(K)[:, None], idx[group]]
    xT_ = mxq(xg, 0, "e4m3")
    w1_ = mxq(f64(w1), 0, "e4m3")
    w2_ = unpack_weight(w2_words, w2_scales, "e2m1")
    h_ = mxq(np.maximum(w1_.T @ xT_, 0.0), 0, "e4m3")
    y = w2_.T @ h_
    return y + f64(b)[:, None]

@@ -1,0 +1,183 @@
+from contextlib import ExitStack
+
+import concourse.mybir as mybir
+
+K, H, M, T, S = 1024, 512, 128, 1024, 512
+FLOPS = 2 * K * H * S + 2 * H * M * S
+
+F32 = mybir.dt.float32
+BF16 = mybir.dt.bfloat16
+I32 = mybir.dt.int32
+U32 = mybir.dt.uint32
+U16 = mybir.dt.uint16
+U8 = mybir.dt.uint8
+FP8X4 = mybir.dt.float8_e4m3fn_x4
+FP4X4 = mybir.dt.float4_e2m1fn_x4
+MULT = mybir.AluOpType.mult
+RELU = mybir.ActivationFunctionType.Relu
+IDENTITY = mybir.ActivationFunctionType.Identity
+
+P = 128
+PACK = 4
+CHUNK = 128
+CHUNKS = S // CHUNK
+
+
+def tile_list_hmlp_bias_kernel(tc, xT, w1, w2_words, w2_scales, wgt, b, offs, out):
+    nc = tc.nc
+    x_planes = xT.rearrange("(a p i) t -> a i p t", p=P, i=PACK)
+    w_rows = w1.rearrange("(a p i) r -> a p i r", p=P, i=PACK)
+
+    with ExitStack() as ctx:
+        keep = ctx.enter_context(tc.tile_pool(name="keep", bufs=1))
+        psum = ctx.enter_context(tc.psum_pool(name="psum", bufs=1))
+
+        def sb(name, cols, dtype):
+            return keep.tile([P, cols], dtype, name=name, align_bytes=64)
+
+        offsets = keep.tile([P, S // 16], U16, name="offsets")
+        weights = sb("weights", S, F32)
+        x_raw = [[sb(f"x_raw{a}{i}", T, F32) for i in range(PACK)] for a in range(2)]
+        w_raw = [sb(f"w_raw{a}", PACK * H, F32) for a in range(2)]
+        picked = [[sb(f"picked{a}{h}", 2 * S, F32) for h in range(2)] for a in range(2)]
+        x_bf = [sb(f"x_bf{a}", PACK * S, BF16) for a in range(2)]
+        w_bf = [sb(f"w_bf{a}", PACK * H, BF16) for a in range(2)]
+        x_codes = [sb(f"x_codes{a}", S, U32) for a in range(2)]
+        x_scales = [sb(f"x_scales{a}", S, U8) for a in range(2)]
+        w_codes = [sb(f"w_codes{a}", H, U32) for a in range(2)]
+        w_scales = [sb(f"w_scales{a}", H, U8) for a in range(2)]
+        h_bf = [sb(f"h_bf{c}", PACK * CHUNK, BF16) for c in range(CHUNKS)]
+        h_codes = [sb(f"h_codes{c}", CHUNK, U32) for c in range(CHUNKS)]
+        h_scales = [sb(f"h_scales{c}", CHUNK, U8) for c in range(CHUNKS)]
+        w2_codes = sb("w2_codes", 2 * M, U8)
+        w2_plane = sb("w2_plane", M, U8)
+        bias = sb("bias", 1, F32)
+        result = [sb(f"result{c}", CHUNK, F32) for c in range(CHUNKS)]
+        h_acc = [psum.tile([P, PACK * CHUNK], F32, name=f"h_acc{c}") for c in range(CHUNKS)]
+        y_acc = [psum.tile([P, CHUNK], F32, name=f"y_acc{c}") for c in range(CHUNKS)]
+
+        def load_x(a, i):
+            nc.sync.dma_start(out=x_raw[a][i][:], in_=x_planes[a, i])
+
+        def load_w(a):
+            nc.sync.dma_start(out=w_raw[a][:], in_=w_rows[a].rearrange("p i r -> p (i r)"))
+
+        nc.sync.dma_start(offsets[:], offs)
+        load_x(0, 0)
+        nc.sync.dma_start(out=weights[:], in_=wgt)
+        for i in range(1, PACK):
+            load_x(0, i)
+        load_w(0)
+        load_x(1, 0)
+        load_w(1)
+        for i in range(1, PACK):
+            load_x(1, i)
+
+        nc.gpsimd.memset(w2_plane[:].bitcast(U32), 0)
+        nc.gpsimd.dma_start(out=w2_codes[:].bitcast(I32), in_=w2_words[0].bitcast(I32))
+        nc.gpsimd.dma_start(out=bias[:], in_=b.rearrange("(p o) -> p o", o=1))
+        for q in range(4):
+            nc.gpsimd.dma_start(
+                out=w2_plane[32 * q : 32 * q + 4, :].bitcast(I32),
+                in_=w2_scales[0, 4 * q : 4 * q + 4, :].bitcast(I32),
+            )
+
+        def copy_on(engine, dst, src):
+            if engine == "scalar":
+                nc.scalar.copy(out=dst, in_=src)
+            else:
+                nc.vector.tensor_copy(out=dst, in_=src)
+
+        def gather(a, i, j0, j1):
+            base = (i % 2) * S
+            nc.vector.tensor_tensor(
+                picked[a][i // 2][:, base + j0 : base + j1],
+                x_raw[a][i][:].indirect(offsets[:, j0 // 16 : j1 // 16]),
+                weights[:, j0:j1],
+                MULT,
+            )
+
+        def weave_x(engine, a, half, j0, j1):
+            src = picked[a][half][:].rearrange("p (e c n) -> p c e n", e=2, n=4)[:, j0 // 4 : j1 // 4]
+            dst = x_bf[a][:].rearrange("p (c n h e) -> p h c e n", n=4, h=2, e=2)[:, half, j0 // 4 : j1 // 4]
+            copy_on(engine, dst, src)
+
+        def weave_w(engine, a):
+            src = w_raw[a][:].rearrange("p (i m t) -> p m i t", i=PACK, t=PACK)
+            dst = w_bf[a][:].rearrange("p (t m i) -> p m i t", t=PACK, i=PACK)
+            copy_on(engine, dst, src)
+
+        def quantize(codes, scales, values, c0, c1):
+            nc.vector.quantize_mx(
+                out=codes[:, c0:c1].bitcast(FP8X4), scales=scales[:, c0:c1], in_=values[:, PACK * c0 : PACK * c1]
+            )
+
+        def first_layer(a, c):
+            cols = slice(c * CHUNK, (c + 1) * CHUNK)
+            for t in range(PACK):
+                rows = slice(t * P, (t + 1) * P)
+                nc.tensor.matmul_mx(
+                    out=h_acc[c][:, t * CHUNK : (t + 1) * CHUNK],
+                    lhsT=w_codes[a][:, rows].bitcast(FP8X4),
+                    lhsT_scale=w_scales[a][:, rows],
+                    rhs=x_codes[a][:, cols].bitcast(FP8X4),
+                    rhs_scale=x_scales[a][:, cols],
+                    start=(a == 0 and t == 0),
+                    stop=(a == 1 and t == PACK - 1),
+                )
+
+        def relu(c):
+            nc.scalar.activation(
+                out=h_bf[c][:].rearrange("p (n t) -> p n t", t=PACK),
+                in_=h_acc[c][:].rearrange("p (t n) -> p n t", t=PACK),
+                func=RELU,
+            )
+
+        def second_layer(c):
+            quantize(h_codes[c], h_scales[c], h_bf[c], 0, CHUNK)
+            nc.tensor.matmul_mx(
+                out=y_acc[c][:],
+                lhsT=w2_codes[:].bitcast(FP4X4),
+                lhsT_scale=w2_plane[:],
+                rhs=h_codes[c][:].bitcast(FP8X4),
+                rhs_scale=h_scales[c][:],
+                start=True,
+                stop=True,
+            )
+
+        def finish(c):
+            nc.scalar.activation(out=result[c][:], in_=y_acc[c][:], func=IDENTITY, bias=bias[:, 0:1])
+            nc.sync.dma_start(out=out[:, c * CHUNK : (c + 1) * CHUNK], in_=result[c][:])
+
+        gather(0, 0, 0, S)
+        gather(0, 1, 0, S)
+        weave_x("scalar", 0, 0, 0, S)
+        gather(0, 2, 0, S)
+        gather(0, 3, 0, S)
+        weave_x("vector", 0, 1, 0, S)
+        weave_w("scalar", 0)
+        quantize(x_codes[0], x_scales[0], x_bf[0], 0, S)
+        gather(1, 0, 0, S)
+        quantize(w_codes[0], w_scales[0], w_bf[0], 0, H)
+        weave_w("scalar", 1)
+        for c in range(CHUNKS):
+            first_layer(0, c)
+        gather(1, 1, 0, S)
+        quantize(w_codes[1], w_scales[1], w_bf[1], 0, H)
+        weave_x("scalar", 1, 0, 0, S)
+        gather(1, 2, 0, S)
+        for step in range(CHUNKS + 4):
+            if step < CHUNKS:
+                gather(1, 3, step * CHUNK, (step + 1) * CHUNK)
+            c = step - 1
+            if 0 <= c < CHUNKS:
+                weave_x("vector", 1, 1, c * CHUNK, (c + 1) * CHUNK)
+            c = step - 2
+            if 0 <= c < CHUNKS:
+                quantize(x_codes[1], x_scales[1], x_bf[1], c * CHUNK, (c + 1) * CHUNK)
+                first_layer(1, c)
+                relu(c)
+            c = step - 4
+            if 0 <= c < CHUNKS:
+                second_layer(c)
+                finish(c)

@@ -21,31 +21,34 @@ P = 128
 PACK = 4
 CHUNK = 128
 CHUNKS = S // CHUNK
+W_SPLIT = 52
 
 
 def tile_list_hmlp_bias_kernel(tc, xT, w1, w2_words, w2_scales, wgt, b, offs, out):
     nc = tc.nc
     x_planes = xT.rearrange("(a p i) t -> a i p t", p=P, i=PACK)
-    w_rows = w1.rearrange("(a p i) r -> a p i r", p=P, i=PACK)
+    w_pairs = w1.rearrange("(a p h e) r -> a h p (e r)", p=P, h=2, e=2)
 
     with ExitStack() as ctx:
         keep = ctx.enter_context(tc.tile_pool(name="keep", bufs=1))
         psum = ctx.enter_context(tc.psum_pool(name="psum", bufs=1))
 
-        def sb(name, cols, dtype):
-            return keep.tile([P, cols], dtype, name=name, align_bytes=64)
+        def sb(name, cols, dtype, tag=None):
+            return keep.tile([P, cols], dtype, name=name, tag=tag or name, align_bytes=64)
 
         offsets = keep.tile([P, S // 16], U16, name="offsets")
         weights = sb("weights", S, F32)
         x_raw = [[sb(f"x_raw{a}{i}", T, F32) for i in range(PACK)] for a in range(2)]
-        w_raw = [sb(f"w_raw{a}", PACK * H, F32) for a in range(2)]
+        w_whole = sb("w_whole", PACK * H, F32)
+        w_raw = [sb("w_raw0", 2 * H, F32), sb("w_raw1", 2 * H, F32, tag="last_w_then_x")]
         picked = [[sb(f"picked{a}{h}", 2 * S, F32) for h in range(2)] for a in range(2)]
-        x_bf = [sb(f"x_bf{a}", PACK * S, BF16) for a in range(2)]
+        x_bf = [sb("x_bf0", PACK * S, BF16), sb("x_bf1", PACK * S, BF16, tag="last_w_then_x")]
         w_bf = [sb(f"w_bf{a}", PACK * H, BF16) for a in range(2)]
         x_codes = [sb(f"x_codes{a}", S, U32) for a in range(2)]
         x_scales = [sb(f"x_scales{a}", S, U8) for a in range(2)]
         w_codes = [sb(f"w_codes{a}", H, U32) for a in range(2)]
-        w_scales = [sb(f"w_scales{a}", H, U8) for a in range(2)]
+        w_planes = sb("w_planes", H, U8)
+        w_scales = [w_planes[4 * a :, :] for a in range(2)]
         h_bf = [sb(f"h_bf{c}", PACK * CHUNK, BF16) for c in range(CHUNKS)]
         h_codes = [sb(f"h_codes{c}", CHUNK, U32) for c in range(CHUNKS)]
         h_scales = [sb(f"h_scales{c}", CHUNK, U8) for c in range(CHUNKS)]
@@ -59,28 +62,29 @@ def tile_list_hmlp_bias_kernel(tc, xT, w1, w2_words, w2_scales, wgt, b, offs, ou
         def load_x(a, i):
             nc.sync.dma_start(out=x_raw[a][i][:], in_=x_planes[a, i])
 
-        def load_w(a):
-            nc.sync.dma_start(out=w_raw[a][:], in_=w_rows[a].rearrange("p i r -> p (i r)"))
+        def load_w(half):
+            nc.sync.dma_start(out=w_raw[half][:], in_=w_pairs[1, half])
 
+        nc.vector.memset(w2_plane[:].bitcast(U32), 0)
         nc.sync.dma_start(offsets[:], offs)
         load_x(0, 0)
         nc.sync.dma_start(out=weights[:], in_=wgt)
         for i in range(1, PACK):
             load_x(0, i)
-        load_w(0)
+        nc.sync.dma_start(out=w_whole[:], in_=w1[0 : P * PACK, :].rearrange("(p i) r -> p (i r)", i=PACK))
         load_x(1, 0)
+        load_w(0)
+        load_x(1, 1)
         load_w(1)
-        for i in range(1, PACK):
-            load_x(1, i)
-
-        nc.gpsimd.memset(w2_plane[:].bitcast(U32), 0)
-        nc.gpsimd.dma_start(out=w2_codes[:].bitcast(I32), in_=w2_words[0].bitcast(I32))
-        nc.gpsimd.dma_start(out=bias[:], in_=b.rearrange("(p o) -> p o", o=1))
+        load_x(1, 2)
+        load_x(1, 3)
+        nc.sync.dma_start(out=w2_codes[:].bitcast(I32), in_=w2_words[0].bitcast(I32))
         for q in range(4):
-            nc.gpsimd.dma_start(
+            nc.sync.dma_start(
                 out=w2_plane[32 * q : 32 * q + 4, :].bitcast(I32),
                 in_=w2_scales[0, 4 * q : 4 * q + 4, :].bitcast(I32),
             )
+        nc.sync.dma_start(out=bias[:], in_=b.rearrange("(p o) -> p o", o=1))
 
         def copy_on(engine, dst, src):
             if engine == "scalar":
@@ -102,9 +106,14 @@ def tile_list_hmlp_bias_kernel(tc, xT, w1, w2_words, w2_scales, wgt, b, offs, ou
             dst = x_bf[a][:].rearrange("p (c n h e) -> p h c e n", n=4, h=2, e=2)[:, half, j0 // 4 : j1 // 4]
             copy_on(engine, dst, src)
 
-        def weave_w(engine, a):
-            src = w_raw[a][:].rearrange("p (i m t) -> p m i t", i=PACK, t=PACK)
-            dst = w_bf[a][:].rearrange("p (t m i) -> p m i t", t=PACK, i=PACK)
+        def weave_w_whole():
+            src = w_whole[:].rearrange("p (i m t) -> p m i t", i=PACK, t=PACK)
+            dst = w_bf[0][:].rearrange("p (t m i) -> p m i t", t=PACK, i=PACK)
+            nc.scalar.copy(out=dst, in_=src)
+
+        def weave_w(engine, half, m0, m1):
+            src = w_raw[half][:].rearrange("p (e m t) -> p m e t", e=2, t=PACK)[:, m0:m1]
+            dst = w_bf[1][:].rearrange("p (t m h e) -> p h m e t", t=PACK, h=2, e=2)[:, half, m0:m1]
             copy_on(engine, dst, src)
 
         def quantize(codes, scales, values, c0, c1):
@@ -126,12 +135,13 @@ def tile_list_hmlp_bias_kernel(tc, xT, w1, w2_words, w2_scales, wgt, b, offs, ou
                     stop=(a == 1 and t == PACK - 1),
                 )
 
-        def relu(c):
-            nc.scalar.activation(
-                out=h_bf[c][:].rearrange("p (n t) -> p n t", t=PACK),
-                in_=h_acc[c][:].rearrange("p (t n) -> p n t", t=PACK),
-                func=RELU,
-            )
+        def relu(engine, c):
+            dst = h_bf[c][:].rearrange("p (n t) -> p n t", t=PACK)
+            src = h_acc[c][:].rearrange("p (t n) -> p n t", t=PACK)
+            if engine == "scalar":
+                nc.scalar.activation(out=dst, in_=src, func=RELU)
+            else:
+                nc.vector.tensor_scalar_max(dst, src, 0.0)
 
         def second_layer(c):
             quantize(h_codes[c], h_scales[c], h_bf[c], 0, CHUNK)
@@ -155,29 +165,28 @@ def tile_list_hmlp_bias_kernel(tc, xT, w1, w2_words, w2_scales, wgt, b, offs, ou
         gather(0, 2, 0, S)
         gather(0, 3, 0, S)
         weave_x("vector", 0, 1, 0, S)
-        weave_w("scalar", 0)
+        weave_w_whole()
         quantize(x_codes[0], x_scales[0], x_bf[0], 0, S)
         gather(1, 0, 0, S)
         quantize(w_codes[0], w_scales[0], w_bf[0], 0, H)
-        weave_w("scalar", 1)
+        weave_w("scalar", 0, 0, P)
+        gather(1, 1, 0, S)
+        weave_w("scalar", 1, 0, W_SPLIT)
+        weave_w("vector", 1, W_SPLIT, P)
+        quantize(w_codes[1], w_scales[1], w_bf[1], 0, H)
         for c in range(CHUNKS):
             first_layer(0, c)
-        gather(1, 1, 0, S)
-        quantize(w_codes[1], w_scales[1], w_bf[1], 0, H)
         weave_x("scalar", 1, 0, 0, S)
         gather(1, 2, 0, S)
-        for step in range(CHUNKS + 4):
-            if step < CHUNKS:
-                gather(1, 3, step * CHUNK, (step + 1) * CHUNK)
-            c = step - 1
-            if 0 <= c < CHUNKS:
-                weave_x("vector", 1, 1, c * CHUNK, (c + 1) * CHUNK)
-            c = step - 2
-            if 0 <= c < CHUNKS:
-                quantize(x_codes[1], x_scales[1], x_bf[1], c * CHUNK, (c + 1) * CHUNK)
-                first_layer(1, c)
-                relu(c)
-            c = step - 4
-            if 0 <= c < CHUNKS:
-                second_layer(c)
-                finish(c)
+        for c in range(CHUNKS):
+            gather(1, 3, c * CHUNK, (c + 1) * CHUNK)
+            weave_x("scalar", 1, 1, c * CHUNK, (c + 1) * CHUNK)
+        for c in range(CHUNKS):
+            quantize(x_codes[1], x_scales[1], x_bf[1], c * CHUNK, (c + 1) * CHUNK)
+            first_layer(1, c)
+        for c in range(CHUNKS):
+            relu("vector" if c == 1 else "scalar", c)
+        for c in range(CHUNKS):
+            second_layer(c)
+        for c in range(CHUNKS):
+            finish(c)

@@ -21,13 +21,13 @@ P = 128
 PACK = 4
 CHUNK = 128
 CHUNKS = S // CHUNK
-W_SPLIT = 52
+W_SPLIT = 24
 
 
 def tile_list_hmlp_bias_kernel(tc, xT, w1, w2_words, w2_scales, wgt, b, offs, out):
     nc = tc.nc
     x_planes = xT.rearrange("(a p i) t -> a i p t", p=P, i=PACK)
-    w_pairs = w1.rearrange("(a p h e) r -> a h p (e r)", p=P, h=2, e=2)
+    w_rows = w1.rearrange("(a p i) r -> a p i r", p=P, i=PACK)
 
     with ExitStack() as ctx:
         keep = ctx.enter_context(tc.tile_pool(name="keep", bufs=1))
@@ -63,7 +63,10 @@ def tile_list_hmlp_bias_kernel(tc, xT, w1, w2_words, w2_scales, wgt, b, offs, ou
             nc.sync.dma_start(out=x_raw[a][i][:], in_=x_planes[a, i])
 
         def load_w(half):
-            nc.sync.dma_start(out=w_raw[half][:], in_=w_pairs[1, half])
+            nc.sync.dma_start(
+                out=w_raw[half][:].rearrange("p (i r) -> p i r", i=PACK),
+                in_=w_rows[1, :, :, half * (H // 2) : (half + 1) * (H // 2)],
+            )
 
         nc.vector.memset(w2_plane[:].bitcast(U32), 0)
         nc.sync.dma_start(offsets[:], offs)
@@ -73,8 +76,8 @@ def tile_list_hmlp_bias_kernel(tc, xT, w1, w2_words, w2_scales, wgt, b, offs, ou
             load_x(0, i)
         nc.sync.dma_start(out=w_whole[:], in_=w1[0 : P * PACK, :].rearrange("(p i) r -> p (i r)", i=PACK))
         load_x(1, 0)
-        load_w(0)
         load_x(1, 1)
+        load_w(0)
         load_w(1)
         load_x(1, 2)
         load_x(1, 3)
@@ -112,8 +115,8 @@ def tile_list_hmlp_bias_kernel(tc, xT, w1, w2_words, w2_scales, wgt, b, offs, ou
             nc.scalar.copy(out=dst, in_=src)
 
         def weave_w(engine, half, m0, m1):
-            src = w_raw[half][:].rearrange("p (e m t) -> p m e t", e=2, t=PACK)[:, m0:m1]
-            dst = w_bf[1][:].rearrange("p (t m h e) -> p h m e t", t=PACK, h=2, e=2)[:, half, m0:m1]
+            src = w_raw[half][:].rearrange("p (i m t) -> p m i t", i=PACK, t=PACK)[:, m0:m1]
+            dst = w_bf[1][:].rearrange("p (t h m i) -> p h m i t", t=PACK, h=2, i=PACK)[:, half, m0:m1]
             copy_on(engine, dst, src)
 
         def quantize(codes, scales, values, c0, c1):
@@ -169,10 +172,10 @@ def tile_list_hmlp_bias_kernel(tc, xT, w1, w2_words, w2_scales, wgt, b, offs, ou
         quantize(x_codes[0], x_scales[0], x_bf[0], 0, S)
         gather(1, 0, 0, S)
         quantize(w_codes[0], w_scales[0], w_bf[0], 0, H)
-        weave_w("scalar", 0, 0, P)
         gather(1, 1, 0, S)
+        weave_w("scalar", 0, 0, P // 2)
         weave_w("scalar", 1, 0, W_SPLIT)
-        weave_w("vector", 1, W_SPLIT, P)
+        weave_w("vector", 1, W_SPLIT, P // 2)
         quantize(w_codes[1], w_scales[1], w_bf[1], 0, H)
         for c in range(CHUNKS):
             first_layer(0, c)

@@ -19,9 +19,14 @@ IDENTITY = mybir.ActivationFunctionType.Identity
 
 P = 128
 PACK = 4
+PASSES = K // (P * PACK)
+LIST_ROWS = 16
+LINE = 4
 CHUNK = 128
 CHUNKS = S // CHUNK
-W_SPLIT = 24
+SCALAR_SHARE_W_PASS0 = 96
+SCALAR_SHARE_W_LAST = 24
+VECTOR_RELU_CHUNK = 1
 
 
 def tile_list_hmlp_bias_kernel(tc, xT, w1, w2_words, w2_scales, wgt, b, offs, out):
@@ -36,24 +41,24 @@ def tile_list_hmlp_bias_kernel(tc, xT, w1, w2_words, w2_scales, wgt, b, offs, ou
         def sb(name, cols, dtype, tag=None):
             return keep.tile([P, cols], dtype, name=name, tag=tag or name, align_bytes=64)
 
-        offsets = keep.tile([P, S // 16], U16, name="offsets")
+        offsets = keep.tile([P, S // LIST_ROWS], U16, name="offsets")
         weights = sb("weights", S, F32)
-        x_raw = [[sb(f"x_raw{a}{i}", T, F32) for i in range(PACK)] for a in range(2)]
-        w_whole = sb("w_whole", PACK * H, F32)
-        w_raw = [sb("w_raw0", 2 * H, F32), sb("w_raw1", 2 * H, F32, tag="last_w_then_x")]
-        picked = [[sb(f"picked{a}{h}", 2 * S, F32) for h in range(2)] for a in range(2)]
+        x_raw = [[sb(f"x_raw{a}{i}", T, F32) for i in range(PACK)] for a in range(PASSES)]
+        w0_raw = sb("w0_raw", PACK * H, F32)
+        w1_raw = [sb("w1_raw0", PACK * H // 2, F32), sb("w1_raw1", PACK * H // 2, F32, tag="last_w_then_x")]
+        picked = [[sb(f"picked{a}{pair}", 2 * S, F32) for pair in range(2)] for a in range(PASSES)]
         x_bf = [sb("x_bf0", PACK * S, BF16), sb("x_bf1", PACK * S, BF16, tag="last_w_then_x")]
-        w_bf = [sb(f"w_bf{a}", PACK * H, BF16) for a in range(2)]
-        x_codes = [sb(f"x_codes{a}", S, U32) for a in range(2)]
-        x_scales = [sb(f"x_scales{a}", S, U8) for a in range(2)]
-        w_codes = [sb(f"w_codes{a}", H, U32) for a in range(2)]
-        w_planes = sb("w_planes", H, U8)
-        w_scales = [w_planes[4 * a :, :] for a in range(2)]
+        w_bf = [sb(f"w_bf{a}", PACK * H, BF16) for a in range(PASSES)]
+        x_codes = [sb(f"x_codes{a}", S, U32) for a in range(PASSES)]
+        x_scales = [sb(f"x_scales{a}", S, U8) for a in range(PASSES)]
+        w_codes = [sb(f"w_codes{a}", H, U32) for a in range(PASSES)]
+        w_scale_tile = sb("w_scale_tile", H, U8)
+        w_scales = [w_scale_tile[4 * a :, :] for a in range(PASSES)]
         h_bf = [sb(f"h_bf{c}", PACK * CHUNK, BF16) for c in range(CHUNKS)]
         h_codes = [sb(f"h_codes{c}", CHUNK, U32) for c in range(CHUNKS)]
         h_scales = [sb(f"h_scales{c}", CHUNK, U8) for c in range(CHUNKS)]
         w2_codes = sb("w2_codes", 2 * M, U8)
-        w2_plane = sb("w2_plane", M, U8)
+        w2_scale_tile = sb("w2_scale_tile", M, U8)
         bias = sb("bias", 1, F32)
         result = [sb(f"result{c}", CHUNK, F32) for c in range(CHUNKS)]
         h_acc = [psum.tile([P, PACK * CHUNK], F32, name=f"h_acc{c}") for c in range(CHUNKS)]
@@ -62,62 +67,53 @@ def tile_list_hmlp_bias_kernel(tc, xT, w1, w2_words, w2_scales, wgt, b, offs, ou
         def load_x(a, i):
             nc.sync.dma_start(out=x_raw[a][i][:], in_=x_planes[a, i])
 
-        def load_w(half):
+        def load_w1_half(half):
             nc.sync.dma_start(
-                out=w_raw[half][:].rearrange("p (i r) -> p i r", i=PACK),
+                out=w1_raw[half][:].rearrange("p (i r) -> p i r", i=PACK),
                 in_=w_rows[1, :, :, half * (H // 2) : (half + 1) * (H // 2)],
             )
 
-        nc.vector.memset(w2_plane[:].bitcast(U32), 0)
-        nc.sync.dma_start(offsets[:], offs)
+        nc.vector.memset(w2_scale_tile[:].bitcast(U32), 0)
+
         load_x(0, 0)
-        nc.sync.dma_start(out=weights[:], in_=wgt)
+        nc.sync.dma_start(offsets[:], offs)
+        nc.scalar.dma_start(out=weights[:], in_=wgt)
         for i in range(1, PACK):
             load_x(0, i)
-        nc.sync.dma_start(out=w_whole[:], in_=w1[0 : P * PACK, :].rearrange("(p i) r -> p (i r)", i=PACK))
         load_x(1, 0)
+        nc.sync.dma_start(out=w0_raw[:], in_=w1[0 : P * PACK, :].rearrange("(p i) r -> p (i r)", i=PACK))
         load_x(1, 1)
-        load_w(0)
-        load_w(1)
+        load_w1_half(0)
+        load_w1_half(1)
         load_x(1, 2)
         load_x(1, 3)
         nc.sync.dma_start(out=w2_codes[:].bitcast(I32), in_=w2_words[0].bitcast(I32))
-        for q in range(4):
+        for quadrant in range(4):
             nc.sync.dma_start(
-                out=w2_plane[32 * q : 32 * q + 4, :].bitcast(I32),
-                in_=w2_scales[0, 4 * q : 4 * q + 4, :].bitcast(I32),
+                out=w2_scale_tile[32 * quadrant : 32 * quadrant + 4, :].bitcast(I32),
+                in_=w2_scales[0, 4 * quadrant : 4 * quadrant + 4, :].bitcast(I32),
             )
         nc.sync.dma_start(out=bias[:], in_=b.rearrange("(p o) -> p o", o=1))
-
-        def copy_on(engine, dst, src):
-            if engine == "scalar":
-                nc.scalar.copy(out=dst, in_=src)
-            else:
-                nc.vector.tensor_copy(out=dst, in_=src)
 
         def gather(a, i, j0, j1):
             base = (i % 2) * S
             nc.vector.tensor_tensor(
                 picked[a][i // 2][:, base + j0 : base + j1],
-                x_raw[a][i][:].indirect(offsets[:, j0 // 16 : j1 // 16]),
+                x_raw[a][i][:].indirect(offsets[:, j0 // LIST_ROWS : j1 // LIST_ROWS]),
                 weights[:, j0:j1],
                 MULT,
             )
 
-        def weave_x(engine, a, half, j0, j1):
-            src = picked[a][half][:].rearrange("p (e c n) -> p c e n", e=2, n=4)[:, j0 // 4 : j1 // 4]
-            dst = x_bf[a][:].rearrange("p (c n h e) -> p h c e n", n=4, h=2, e=2)[:, half, j0 // 4 : j1 // 4]
-            copy_on(engine, dst, src)
-
-        def weave_w_whole():
-            src = w_whole[:].rearrange("p (i m t) -> p m i t", i=PACK, t=PACK)
-            dst = w_bf[0][:].rearrange("p (t m i) -> p m i t", t=PACK, i=PACK)
+        def weave_x(a, pair, j0, j1):
+            lines = slice(j0 // LINE, j1 // LINE)
+            src = picked[a][pair][:].rearrange("p (e c n) -> p c e n", e=2, n=LINE)[:, lines]
+            dst = x_bf[a][:].rearrange("p (c n h e) -> p h c e n", n=LINE, h=2, e=2)[:, pair, lines]
             nc.scalar.copy(out=dst, in_=src)
 
-        def weave_w(engine, half, m0, m1):
-            src = w_raw[half][:].rearrange("p (i m t) -> p m i t", i=PACK, t=PACK)[:, m0:m1]
-            dst = w_bf[1][:].rearrange("p (t h m i) -> p h m i t", t=PACK, h=2, i=PACK)[:, half, m0:m1]
-            copy_on(engine, dst, src)
+        def weave_w(copy, raw, a, m_first, m0, m1):
+            src = raw[:].rearrange("p (i m t) -> p m i t", i=PACK, t=PACK)[:, m0:m1]
+            dst = w_bf[a][:].rearrange("p (t m i) -> p m i t", t=PACK, i=PACK)[:, m_first + m0 : m_first + m1]
+            copy(out=dst, in_=src)
 
         def quantize(codes, scales, values, c0, c1):
             nc.vector.quantize_mx(
@@ -135,23 +131,23 @@ def tile_list_hmlp_bias_kernel(tc, xT, w1, w2_words, w2_scales, wgt, b, offs, ou
                     rhs=x_codes[a][:, cols].bitcast(FP8X4),
                     rhs_scale=x_scales[a][:, cols],
                     start=(a == 0 and t == 0),
-                    stop=(a == 1 and t == PACK - 1),
+                    stop=(a == PASSES - 1 and t == PACK - 1),
                 )
 
-        def relu(engine, c):
+        def relu(c):
             dst = h_bf[c][:].rearrange("p (n t) -> p n t", t=PACK)
             src = h_acc[c][:].rearrange("p (t n) -> p n t", t=PACK)
-            if engine == "scalar":
-                nc.scalar.activation(out=dst, in_=src, func=RELU)
-            else:
+            if c == VECTOR_RELU_CHUNK:
                 nc.vector.tensor_scalar_max(dst, src, 0.0)
+            else:
+                nc.scalar.activation(out=dst, in_=src, func=RELU)
 
         def second_layer(c):
             quantize(h_codes[c], h_scales[c], h_bf[c], 0, CHUNK)
             nc.tensor.matmul_mx(
                 out=y_acc[c][:],
                 lhsT=w2_codes[:].bitcast(FP4X4),
-                lhsT_scale=w2_plane[:],
+                lhsT_scale=w2_scale_tile[:],
                 rhs=h_codes[c][:].bitcast(FP8X4),
                 rhs_scale=h_scales[c][:],
                 start=True,
@@ -164,31 +160,33 @@ def tile_list_hmlp_bias_kernel(tc, xT, w1, w2_words, w2_scales, wgt, b, offs, ou
 
         gather(0, 0, 0, S)
         gather(0, 1, 0, S)
-        weave_x("scalar", 0, 0, 0, S)
+        weave_x(0, 0, 0, S)
         gather(0, 2, 0, S)
         gather(0, 3, 0, S)
-        weave_x("vector", 0, 1, 0, S)
-        weave_w_whole()
-        quantize(x_codes[0], x_scales[0], x_bf[0], 0, S)
+        weave_x(0, 1, 0, S)
         gather(1, 0, 0, S)
-        quantize(w_codes[0], w_scales[0], w_bf[0], 0, H)
+        weave_w(nc.scalar.copy, w0_raw, 0, 0, 0, SCALAR_SHARE_W_PASS0)
+        weave_w(nc.vector.tensor_copy, w0_raw, 0, 0, SCALAR_SHARE_W_PASS0, P)
+        quantize(x_codes[0], x_scales[0], x_bf[0], 0, S)
         gather(1, 1, 0, S)
-        weave_w("scalar", 0, 0, P // 2)
-        weave_w("scalar", 1, 0, W_SPLIT)
-        weave_w("vector", 1, W_SPLIT, P // 2)
+        quantize(w_codes[0], w_scales[0], w_bf[0], 0, H)
+        weave_w(nc.scalar.copy, w1_raw[0], 1, 0, 0, P // 2)
+        weave_w(nc.scalar.copy, w1_raw[1], 1, P // 2, 0, SCALAR_SHARE_W_LAST)
+        weave_w(nc.vector.tensor_copy, w1_raw[1], 1, P // 2, SCALAR_SHARE_W_LAST, P // 2)
         quantize(w_codes[1], w_scales[1], w_bf[1], 0, H)
         for c in range(CHUNKS):
             first_layer(0, c)
-        weave_x("scalar", 1, 0, 0, S)
+        weave_x(1, 0, 0, S)
         gather(1, 2, 0, S)
+
         for c in range(CHUNKS):
             gather(1, 3, c * CHUNK, (c + 1) * CHUNK)
-            weave_x("scalar", 1, 1, c * CHUNK, (c + 1) * CHUNK)
+            weave_x(1, 1, c * CHUNK, (c + 1) * CHUNK)
         for c in range(CHUNKS):
             quantize(x_codes[1], x_scales[1], x_bf[1], c * CHUNK, (c + 1) * CHUNK)
             first_layer(1, c)
         for c in range(CHUNKS):
-            relu("vector" if c == 1 else "scalar", c)
+            relu(c)
         for c in range(CHUNKS):
             second_layer(c)
         for c in range(CHUNKS):

@@ -22,6 +22,7 @@ PACK = 4
 PASSES = K // (P * PACK)
 LIST_ROWS = 16
 LINE = 4
+BLOCK = 32
 CHUNK = 128
 CHUNKS = S // CHUNK
 SCALAR_SHARE_W_PASS0 = 96
@@ -43,6 +44,9 @@ def tile_list_hmlp_bias_kernel(tc, xT, w1, w2_words, w2_scales, wgt, b, offs, ou
 
         offsets = keep.tile([P, S // LIST_ROWS], U16, name="offsets")
         weights = sb("weights", S, F32)
+        wgt_runs = sb("wgt_runs", BLOCK, F32)
+        wgt_turned = sb("wgt_turned", BLOCK, F32)
+        wgt_repeated = sb("wgt_repeated", S, F32)
         x_raw = [[sb(f"x_raw{a}{i}", T, F32) for i in range(PACK)] for a in range(PASSES)]
         w0_raw = sb("w0_raw", PACK * H, F32)
         w1_raw = [sb("w1_raw0", PACK * H // 2, F32), sb("w1_raw1", PACK * H // 2, F32, tag="last_w_then_x")]
@@ -75,9 +79,11 @@ def tile_list_hmlp_bias_kernel(tc, xT, w1, w2_words, w2_scales, wgt, b, offs, ou
 
         nc.vector.memset(w2_scale_tile[:].bitcast(U32), 0)
 
+        nc.sync.dma_start(
+            out=wgt_runs[:], in_=wgt.rearrange("(g u) (c n) -> g u c n", u=LIST_ROWS, n=BLOCK)[:, 0]
+        )
         load_x(0, 0)
         nc.sync.dma_start(offsets[:], offs)
-        nc.scalar.dma_start(out=weights[:], in_=wgt)
         for i in range(1, PACK):
             load_x(0, i)
         load_x(1, 0)
@@ -157,6 +163,13 @@ def tile_list_hmlp_bias_kernel(tc, xT, w1, w2_words, w2_scales, wgt, b, offs, ou
         def finish(c):
             nc.scalar.activation(out=result[c][:], in_=y_acc[c][:], func=IDENTITY, bias=bias[:, 0:1])
             nc.sync.dma_start(out=out[:, c * CHUNK : (c + 1) * CHUNK], in_=result[c][:])
+
+        nc.vector.transpose(wgt_turned[:], wgt_runs[:])
+        nc.vector.tensor_copy(
+            out=wgt_repeated[:].rearrange("p (c h u) -> p c h u", h=2, u=LIST_ROWS),
+            in_=wgt_turned[:].rearrange("p (h c) -> p c h", h=2).unsqueeze(3).to_broadcast([P, LIST_ROWS, 2, LIST_ROWS]),
+        )
+        nc.vector.transpose(weights[:], wgt_repeated[:])
 
         gather(0, 0, 0, S)
         gather(0, 1, 0, S)

@@ -25,7 +25,6 @@ LINE = 4
 BLOCK = 32
 CHUNK = 128
 CHUNKS = S // CHUNK
-SCALAR_SHARE_W_PASS0 = 96
 SCALAR_SHARE_W_LAST = 24
 VECTOR_RELU_CHUNK = 1
 
@@ -86,8 +85,8 @@ def tile_list_hmlp_bias_kernel(tc, xT, w1, w2_words, w2_scales, wgt, b, offs, ou
         nc.sync.dma_start(offsets[:], offs)
         for i in range(1, PACK):
             load_x(0, i)
-        load_x(1, 0)
         nc.sync.dma_start(out=w0_raw[:], in_=w1[0 : P * PACK, :].rearrange("(p i) r -> p (i r)", i=PACK))
+        load_x(1, 0)
         load_x(1, 1)
         load_w1_half(0)
         load_w1_half(1)
@@ -110,11 +109,11 @@ def tile_list_hmlp_bias_kernel(tc, xT, w1, w2_words, w2_scales, wgt, b, offs, ou
                 MULT,
             )
 
-        def weave_x(a, pair, j0, j1):
+        def weave_x(copy, a, pair, j0, j1):
             lines = slice(j0 // LINE, j1 // LINE)
             src = picked[a][pair][:].rearrange("p (e c n) -> p c e n", e=2, n=LINE)[:, lines]
             dst = x_bf[a][:].rearrange("p (c n h e) -> p h c e n", n=LINE, h=2, e=2)[:, pair, lines]
-            nc.scalar.copy(out=dst, in_=src)
+            copy(out=dst, in_=src)
 
         def weave_w(copy, raw, a, m_first, m0, m1):
             src = raw[:].rearrange("p (i m t) -> p m i t", i=PACK, t=PACK)[:, m0:m1]
@@ -165,22 +164,27 @@ def tile_list_hmlp_bias_kernel(tc, xT, w1, w2_words, w2_scales, wgt, b, offs, ou
             nc.sync.dma_start(out=out[:, c * CHUNK : (c + 1) * CHUNK], in_=result[c][:])
 
         nc.vector.transpose(wgt_turned[:], wgt_runs[:])
-        nc.vector.tensor_copy(
-            out=wgt_repeated[:].rearrange("p (c h u) -> p c h u", h=2, u=LIST_ROWS),
-            in_=wgt_turned[:].rearrange("p (h c) -> p c h", h=2).unsqueeze(3).to_broadcast([P, LIST_ROWS, 2, LIST_ROWS]),
-        )
-        nc.vector.transpose(weights[:], wgt_repeated[:])
+        repeated = wgt_repeated[:].rearrange("p (c h u) -> p c h u", h=2, u=LIST_ROWS)
+        turned = wgt_turned[:].rearrange("p (h c) -> p c h", h=2).unsqueeze(3)
+        halves = [slice(half * S // 2, (half + 1) * S // 2) for half in range(2)]
+        for half in range(2):
+            runs = slice(half * LIST_ROWS // 2, (half + 1) * LIST_ROWS // 2)
+            nc.vector.tensor_copy(
+                out=repeated[:, runs], in_=turned[:, runs].to_broadcast([P, LIST_ROWS // 2, 2, LIST_ROWS])
+            )
+        for half in halves:
+            nc.vector.transpose(weights[:, half], wgt_repeated[:, half])
 
-        gather(0, 0, 0, S)
+        for half in halves:
+            gather(0, 0, half.start, half.stop)
         gather(0, 1, 0, S)
-        weave_x(0, 0, 0, S)
+        weave_x(nc.scalar.copy, 0, 0, 0, S)
         gather(0, 2, 0, S)
         gather(0, 3, 0, S)
-        weave_x(0, 1, 0, S)
-        gather(1, 0, 0, S)
-        weave_w(nc.scalar.copy, w0_raw, 0, 0, 0, SCALAR_SHARE_W_PASS0)
-        weave_w(nc.vector.tensor_copy, w0_raw, 0, 0, SCALAR_SHARE_W_PASS0, P)
+        weave_x(nc.vector.tensor_copy, 0, 1, 0, S)
+        weave_w(nc.scalar.copy, w0_raw, 0, 0, 0, P)
         quantize(x_codes[0], x_scales[0], x_bf[0], 0, S)
+        gather(1, 0, 0, S)
         gather(1, 1, 0, S)
         quantize(w_codes[0], w_scales[0], w_bf[0], 0, H)
         weave_w(nc.scalar.copy, w1_raw[0], 1, 0, 0, P // 2)
@@ -189,12 +193,12 @@ def tile_list_hmlp_bias_kernel(tc, xT, w1, w2_words, w2_scales, wgt, b, offs, ou
         quantize(w_codes[1], w_scales[1], w_bf[1], 0, H)
         for c in range(CHUNKS):
             first_layer(0, c)
-        weave_x(1, 0, 0, S)
+        weave_x(nc.scalar.copy, 1, 0, 0, S)
         gather(1, 2, 0, S)
 
         for c in range(CHUNKS):
             gather(1, 3, c * CHUNK, (c + 1) * CHUNK)
-            weave_x(1, 1, c * CHUNK, (c + 1) * CHUNK)
+            weave_x(nc.scalar.copy, 1, 1, c * CHUNK, (c + 1) * CHUNK)
         for c in range(CHUNKS):
             quantize(x_codes[1], x_scales[1], x_bf[1], c * CHUNK, (c + 1) * CHUNK)
             first_layer(1, c)

@@ -25,14 +25,14 @@ LINE = 4
 BLOCK = 32
 CHUNK = 128
 CHUNKS = S // CHUNK
-SCALAR_SHARE_W_LAST = 24
+SCALAR_SHARE_W = (96, 44)
 VECTOR_RELU_CHUNK = 1
 
 
 def tile_list_hmlp_bias_kernel(tc, xT, w1, w2_words, w2_scales, wgt, b, offs, out):
     nc = tc.nc
     x_planes = xT.rearrange("(a p i) t -> a i p t", p=P, i=PACK)
-    w_rows = w1.rearrange("(a p i) r -> a p i r", p=P, i=PACK)
+    w_rows = w1.rearrange("(a p i) r -> a p (i r)", p=P, i=PACK)
 
     with ExitStack() as ctx:
         keep = ctx.enter_context(tc.tile_pool(name="keep", bufs=1))
@@ -47,8 +47,7 @@ def tile_list_hmlp_bias_kernel(tc, xT, w1, w2_words, w2_scales, wgt, b, offs, ou
         wgt_turned = sb("wgt_turned", BLOCK, F32)
         wgt_repeated = sb("wgt_repeated", S, F32)
         x_raw = [[sb(f"x_raw{a}{i}", T, F32) for i in range(PACK)] for a in range(PASSES)]
-        w0_raw = sb("w0_raw", PACK * H, F32)
-        w1_raw = [sb("w1_raw0", PACK * H // 2, F32), sb("w1_raw1", PACK * H // 2, F32, tag="last_w_then_x")]
+        w_raw = [sb("w_raw0", PACK * H, F32), sb("w_raw1", PACK * H, F32, tag="last_w_then_x")]
         picked = [[sb(f"picked{a}{pair}", 2 * S, F32) for pair in range(2)] for a in range(PASSES)]
         x_bf = [sb("x_bf0", PACK * S, BF16), sb("x_bf1", PACK * S, BF16, tag="last_w_then_x")]
         w_bf = [sb(f"w_bf{a}", PACK * H, BF16) for a in range(PASSES)]
@@ -70,11 +69,8 @@ def tile_list_hmlp_bias_kernel(tc, xT, w1, w2_words, w2_scales, wgt, b, offs, ou
         def load_x(a, i):
             nc.sync.dma_start(out=x_raw[a][i][:], in_=x_planes[a, i])
 
-        def load_w1_half(half):
-            nc.sync.dma_start(
-                out=w1_raw[half][:].rearrange("p (i r) -> p i r", i=PACK),
-                in_=w_rows[1, :, :, half * (H // 2) : (half + 1) * (H // 2)],
-            )
+        def load_w(a):
+            nc.sync.dma_start(out=w_raw[a][:], in_=w_rows[a])
 
         nc.vector.memset(w2_scale_tile[:].bitcast(U32), 0)
 
@@ -85,11 +81,10 @@ def tile_list_hmlp_bias_kernel(tc, xT, w1, w2_words, w2_scales, wgt, b, offs, ou
         nc.sync.dma_start(offsets[:], offs)
         for i in range(1, PACK):
             load_x(0, i)
-        nc.sync.dma_start(out=w0_raw[:], in_=w1[0 : P * PACK, :].rearrange("(p i) r -> p (i r)", i=PACK))
         load_x(1, 0)
+        load_w(0)
         load_x(1, 1)
-        load_w1_half(0)
-        load_w1_half(1)
+        load_w(1)
         load_x(1, 2)
         load_x(1, 3)
         nc.sync.dma_start(out=w2_codes[:].bitcast(I32), in_=w2_words[0].bitcast(I32))
@@ -115,9 +110,9 @@ def tile_list_hmlp_bias_kernel(tc, xT, w1, w2_words, w2_scales, wgt, b, offs, ou
             dst = x_bf[a][:].rearrange("p (c n h e) -> p h c e n", n=LINE, h=2, e=2)[:, pair, lines]
             copy(out=dst, in_=src)
 
-        def weave_w(copy, raw, a, m_first, m0, m1):
-            src = raw[:].rearrange("p (i m t) -> p m i t", i=PACK, t=PACK)[:, m0:m1]
-            dst = w_bf[a][:].rearrange("p (t m i) -> p m i t", t=PACK, i=PACK)[:, m_first + m0 : m_first + m1]
+        def weave_w(copy, a, m0, m1):
+            src = w_raw[a][:].rearrange("p (i m t) -> p m i t", i=PACK, t=PACK)[:, m0:m1]
+            dst = w_bf[a][:].rearrange("p (t m i) -> p m i t", t=PACK, i=PACK)[:, m0:m1]
             copy(out=dst, in_=src)
 
         def quantize(codes, scales, values, c0, c1):
@@ -181,15 +176,15 @@ def tile_list_hmlp_bias_kernel(tc, xT, w1, w2_words, w2_scales, wgt, b, offs, ou
         weave_x(nc.scalar.copy, 0, 0, 0, S)
         gather(0, 2, 0, S)
         gather(0, 3, 0, S)
-        weave_x(nc.vector.tensor_copy, 0, 1, 0, S)
-        weave_w(nc.scalar.copy, w0_raw, 0, 0, 0, P)
-        quantize(x_codes[0], x_scales[0], x_bf[0], 0, S)
+        weave_x(nc.scalar.copy, 0, 1, 0, S)
         gather(1, 0, 0, S)
+        weave_w(nc.scalar.copy, 0, 0, SCALAR_SHARE_W[0])
+        weave_w(nc.vector.tensor_copy, 0, SCALAR_SHARE_W[0], P)
+        quantize(x_codes[0], x_scales[0], x_bf[0], 0, S)
         gather(1, 1, 0, S)
         quantize(w_codes[0], w_scales[0], w_bf[0], 0, H)
-        weave_w(nc.scalar.copy, w1_raw[0], 1, 0, 0, P // 2)
-        weave_w(nc.scalar.copy, w1_raw[1], 1, P // 2, 0, SCALAR_SHARE_W_LAST)
-        weave_w(nc.vector.tensor_copy, w1_raw[1], 1, P // 2, SCALAR_SHARE_W_LAST, P // 2)
+        weave_w(nc.scalar.copy, 1, 0, SCALAR_SHARE_W[1])
+        weave_w(nc.vector.tensor_copy, 1, SCALAR_SHARE_W[1], P)
         quantize(w_codes[1], w_scales[1], w_bf[1], 0, H)
         for c in range(CHUNKS):
             first_layer(0, c)

@@ -25,14 +25,15 @@ LINE = 4
 BLOCK = 32
 CHUNK = 128
 CHUNKS = S // CHUNK
-SCALAR_SHARE_W = (96, 44)
-VECTOR_RELU_CHUNK = 1
+SCALAR_SHARE_W = (72, 100)
+VECTOR_RELU_CHUNK = (0, 2)
 
 
 def tile_list_hmlp_bias_kernel(tc, xT, w1, w2_words, w2_scales, wgt, b, offs, out):
     nc = tc.nc
     x_planes = xT.rearrange("(a p i) t -> a i p t", p=P, i=PACK)
-    w_rows = w1.rearrange("(a p i) r -> a p (i r)", p=P, i=PACK)
+    w_rows = w1.rearrange("(a p i) r -> a p i r", p=P, i=PACK)
+    w_pieces = ((0, 0, P), (1, 0, P))
 
     with ExitStack() as ctx:
         keep = ctx.enter_context(tc.tile_pool(name="keep", bufs=1))
@@ -47,15 +48,14 @@ def tile_list_hmlp_bias_kernel(tc, xT, w1, w2_words, w2_scales, wgt, b, offs, ou
         wgt_turned = sb("wgt_turned", BLOCK, F32)
         wgt_repeated = sb("wgt_repeated", S, F32)
         x_raw = [[sb(f"x_raw{a}{i}", T, F32) for i in range(PACK)] for a in range(PASSES)]
-        w_raw = [sb("w_raw0", PACK * H, F32), sb("w_raw1", PACK * H, F32, tag="last_w_then_x")]
+        w_raw = [sb(f"w_raw{a}", PACK * H, F32) for a in range(PASSES)]
         picked = [[sb(f"picked{a}{pair}", 2 * S, F32) for pair in range(2)] for a in range(PASSES)]
-        x_bf = [sb("x_bf0", PACK * S, BF16), sb("x_bf1", PACK * S, BF16, tag="last_w_then_x")]
+        x_bf = [sb(f"x_bf{a}", PACK * S, BF16) for a in range(PASSES)]
         w_bf = [sb(f"w_bf{a}", PACK * H, BF16) for a in range(PASSES)]
-        x_codes = [sb(f"x_codes{a}", S, U32) for a in range(PASSES)]
+        x_codes = [sb("x_codes0", S, U32, tag="x_raw12"), sb("x_codes1", S, U32)]
         x_scales = [sb(f"x_scales{a}", S, U8) for a in range(PASSES)]
         w_codes = [sb(f"w_codes{a}", H, U32) for a in range(PASSES)]
-        w_scale_tile = sb("w_scale_tile", H, U8)
-        w_scales = [w_scale_tile[4 * a :, :] for a in range(PASSES)]
+        w_scales = [sb(f"w_scales{a}", H, U8) for a in range(PASSES)]
         h_bf = [sb(f"h_bf{c}", PACK * CHUNK, BF16) for c in range(CHUNKS)]
         h_codes = [sb(f"h_codes{c}", CHUNK, U32) for c in range(CHUNKS)]
         h_scales = [sb(f"h_scales{c}", CHUNK, U8) for c in range(CHUNKS)]
@@ -69,8 +69,12 @@ def tile_list_hmlp_bias_kernel(tc, xT, w1, w2_words, w2_scales, wgt, b, offs, ou
         def load_x(a, i):
             nc.sync.dma_start(out=x_raw[a][i][:], in_=x_planes[a, i])
 
-        def load_w(a):
-            nc.sync.dma_start(out=w_raw[a][:], in_=w_rows[a])
+        def load_w(piece):
+            a, m0, count = w_pieces[piece]
+            nc.sync.dma_start(
+                out=w_raw[piece][:].rearrange("p (i r) -> p i r", i=PACK),
+                in_=w_rows[a, :, :, PACK * m0 : PACK * (m0 + count)],
+            )
 
         nc.vector.memset(w2_scale_tile[:].bitcast(U32), 0)
 
@@ -79,13 +83,14 @@ def tile_list_hmlp_bias_kernel(tc, xT, w1, w2_words, w2_scales, wgt, b, offs, ou
         )
         load_x(0, 0)
         nc.sync.dma_start(offsets[:], offs)
-        for i in range(1, PACK):
-            load_x(0, i)
+        load_x(0, 1)
+        load_x(0, 2)
+        load_x(0, 3)
         load_x(1, 0)
         load_w(0)
         load_x(1, 1)
-        load_w(1)
         load_x(1, 2)
+        load_w(1)
         load_x(1, 3)
         nc.sync.dma_start(out=w2_codes[:].bitcast(I32), in_=w2_words[0].bitcast(I32))
         for quadrant in range(4):
@@ -95,7 +100,7 @@ def tile_list_hmlp_bias_kernel(tc, xT, w1, w2_words, w2_scales, wgt, b, offs, ou
             )
         nc.sync.dma_start(out=bias[:], in_=b.rearrange("(p o) -> p o", o=1))
 
-        def gather(a, i, j0, j1):
+        def gather(a, i, j0=0, j1=S):
             base = (i % 2) * S
             nc.vector.tensor_tensor(
                 picked[a][i // 2][:, base + j0 : base + j1],
@@ -104,21 +109,32 @@ def tile_list_hmlp_bias_kernel(tc, xT, w1, w2_words, w2_scales, wgt, b, offs, ou
                 MULT,
             )
 
-        def weave_x(copy, a, pair, j0, j1):
+        def weave_x(a, pair, j0=0, j1=S):
             lines = slice(j0 // LINE, j1 // LINE)
             src = picked[a][pair][:].rearrange("p (e c n) -> p c e n", e=2, n=LINE)[:, lines]
             dst = x_bf[a][:].rearrange("p (c n h e) -> p h c e n", n=LINE, h=2, e=2)[:, pair, lines]
-            copy(out=dst, in_=src)
+            nc.scalar.copy(out=dst, in_=src)
 
-        def weave_w(copy, a, m0, m1):
-            src = w_raw[a][:].rearrange("p (i m t) -> p m i t", i=PACK, t=PACK)[:, m0:m1]
-            dst = w_bf[a][:].rearrange("p (t m i) -> p m i t", t=PACK, i=PACK)[:, m0:m1]
-            copy(out=dst, in_=src)
+        def weave_w(piece):
+            a, m0, count = w_pieces[piece]
+            src = w_raw[piece][:].rearrange("p (i m t) -> p m i t", i=PACK, t=PACK)
+            dst = w_bf[a][:].rearrange("p (t m i) -> p m i t", t=PACK, i=PACK)[:, m0 : m0 + count]
+            share = SCALAR_SHARE_W[piece]
+            nc.scalar.copy(out=dst[:, :share], in_=src[:, :share])
+            if share < count:
+                nc.vector.tensor_copy(out=dst[:, share:], in_=src[:, share:])
 
         def quantize(codes, scales, values, c0, c1):
             nc.vector.quantize_mx(
                 out=codes[:, c0:c1].bitcast(FP8X4), scales=scales[:, c0:c1], in_=values[:, PACK * c0 : PACK * c1]
             )
+
+        def quantize_x_chunk(c):
+            quantize(x_codes[1], x_scales[1], x_bf[1], c * CHUNK, (c + 1) * CHUNK)
+
+        def last_plane(c):
+            gather(1, 3, c * CHUNK, (c + 1) * CHUNK)
+            weave_x(1, 1, c * CHUNK, (c + 1) * CHUNK)
 
         def first_layer(a, c):
             cols = slice(c * CHUNK, (c + 1) * CHUNK)
@@ -137,7 +153,7 @@ def tile_list_hmlp_bias_kernel(tc, xT, w1, w2_words, w2_scales, wgt, b, offs, ou
         def relu(c):
             dst = h_bf[c][:].rearrange("p (n t) -> p n t", t=PACK)
             src = h_acc[c][:].rearrange("p (t n) -> p n t", t=PACK)
-            if c == VECTOR_RELU_CHUNK:
+            if c in VECTOR_RELU_CHUNK:
                 nc.vector.tensor_scalar_max(dst, src, 0.0)
             else:
                 nc.scalar.activation(out=dst, in_=src, func=RELU)
@@ -172,30 +188,29 @@ def tile_list_hmlp_bias_kernel(tc, xT, w1, w2_words, w2_scales, wgt, b, offs, ou
 
         for half in halves:
             gather(0, 0, half.start, half.stop)
-        gather(0, 1, 0, S)
-        weave_x(nc.scalar.copy, 0, 0, 0, S)
-        gather(0, 2, 0, S)
-        gather(0, 3, 0, S)
-        weave_x(nc.scalar.copy, 0, 1, 0, S)
-        gather(1, 0, 0, S)
-        weave_w(nc.scalar.copy, 0, 0, SCALAR_SHARE_W[0])
-        weave_w(nc.vector.tensor_copy, 0, SCALAR_SHARE_W[0], P)
-        quantize(x_codes[0], x_scales[0], x_bf[0], 0, S)
-        gather(1, 1, 0, S)
+        gather(0, 1)
+        weave_x(0, 0)
+        gather(0, 2)
+        gather(0, 3)
+        weave_x(0, 1)
+        gather(1, 0)
+        weave_w(0)
+        gather(1, 1)
         quantize(w_codes[0], w_scales[0], w_bf[0], 0, H)
-        weave_w(nc.scalar.copy, 1, 0, SCALAR_SHARE_W[1])
-        weave_w(nc.vector.tensor_copy, 1, SCALAR_SHARE_W[1], P)
-        quantize(w_codes[1], w_scales[1], w_bf[1], 0, H)
+        weave_x(1, 0)
+        gather(1, 2)
+        weave_w(1)
+        quantize(x_codes[0], x_scales[0], x_bf[0], 0, S)
         for c in range(CHUNKS):
             first_layer(0, c)
-        weave_x(nc.scalar.copy, 1, 0, 0, S)
-        gather(1, 2, 0, S)
-
         for c in range(CHUNKS):
-            gather(1, 3, c * CHUNK, (c + 1) * CHUNK)
-            weave_x(nc.scalar.copy, 1, 1, c * CHUNK, (c + 1) * CHUNK)
-        for c in range(CHUNKS):
-            quantize(x_codes[1], x_scales[1], x_bf[1], c * CHUNK, (c + 1) * CHUNK)
+            last_plane(c)
+        quantize_x_chunk(0)
+        for half in range(2):
+            quantize(w_codes[1], w_scales[1], w_bf[1], half * H // 2, (half + 1) * H // 2)
+        first_layer(1, 0)
+        for c in range(1, CHUNKS):
+            quantize_x_chunk(c)
             first_layer(1, c)
         for c in range(CHUNKS):
             relu(c)

@@ -26,14 +26,14 @@ BLOCK = 32
 CHUNK = 128
 CHUNKS = S // CHUNK
 SCALAR_SHARE_W = (72, 100)
-VECTOR_RELU_CHUNK = (0, 2)
+VECTOR_RELU_CHUNKS = (0, 2)
 
 
 def tile_list_hmlp_bias_kernel(tc, xT, w1, w2_words, w2_scales, wgt, b, offs, out):
     nc = tc.nc
     x_planes = xT.rearrange("(a p i) t -> a i p t", p=P, i=PACK)
-    w_rows = w1.rearrange("(a p i) r -> a p i r", p=P, i=PACK)
-    w_pieces = ((0, 0, P), (1, 0, P))
+    w_rows = w1.rearrange("(a p i) r -> a p (i r)", p=P, i=PACK)
+    wgt_once = wgt.rearrange("p (h j) -> (p h) j", h=2)[:: LIST_ROWS + 1]
 
     with ExitStack() as ctx:
         keep = ctx.enter_context(tc.tile_pool(name="keep", bufs=1))
@@ -69,23 +69,16 @@ def tile_list_hmlp_bias_kernel(tc, xT, w1, w2_words, w2_scales, wgt, b, offs, ou
         def load_x(a, i):
             nc.sync.dma_start(out=x_raw[a][i][:], in_=x_planes[a, i])
 
-        def load_w(piece):
-            a, m0, count = w_pieces[piece]
-            nc.sync.dma_start(
-                out=w_raw[piece][:].rearrange("p (i r) -> p i r", i=PACK),
-                in_=w_rows[a, :, :, PACK * m0 : PACK * (m0 + count)],
-            )
+        def load_w(a):
+            nc.sync.dma_start(out=w_raw[a][:], in_=w_rows[a])
 
         nc.vector.memset(w2_scale_tile[:].bitcast(U32), 0)
 
-        nc.sync.dma_start(
-            out=wgt_runs[:], in_=wgt.rearrange("(g u) (c n) -> g u c n", u=LIST_ROWS, n=BLOCK)[:, 0]
-        )
+        nc.sync.dma_start(out=wgt_runs[:], in_=wgt_once.rearrange("e (c n) -> e c n", n=BLOCK))
         load_x(0, 0)
         nc.sync.dma_start(offsets[:], offs)
-        load_x(0, 1)
-        load_x(0, 2)
-        load_x(0, 3)
+        for i in range(1, PACK):
+            load_x(0, i)
         load_x(1, 0)
         load_w(0)
         load_x(1, 1)
@@ -115,14 +108,12 @@ def tile_list_hmlp_bias_kernel(tc, xT, w1, w2_words, w2_scales, wgt, b, offs, ou
             dst = x_bf[a][:].rearrange("p (c n h e) -> p h c e n", n=LINE, h=2, e=2)[:, pair, lines]
             nc.scalar.copy(out=dst, in_=src)
 
-        def weave_w(piece):
-            a, m0, count = w_pieces[piece]
-            src = w_raw[piece][:].rearrange("p (i m t) -> p m i t", i=PACK, t=PACK)
-            dst = w_bf[a][:].rearrange("p (t m i) -> p m i t", t=PACK, i=PACK)[:, m0 : m0 + count]
-            share = SCALAR_SHARE_W[piece]
+        def weave_w(a):
+            src = w_raw[a][:].rearrange("p (i m t) -> p m i t", i=PACK, t=PACK)
+            dst = w_bf[a][:].rearrange("p (t m i) -> p m i t", t=PACK, i=PACK)
+            share = SCALAR_SHARE_W[a]
             nc.scalar.copy(out=dst[:, :share], in_=src[:, :share])
-            if share < count:
-                nc.vector.tensor_copy(out=dst[:, share:], in_=src[:, share:])
+            nc.vector.tensor_copy(out=dst[:, share:], in_=src[:, share:])
 
         def quantize(codes, scales, values, c0, c1):
             nc.vector.quantize_mx(
@@ -153,7 +144,7 @@ def tile_list_hmlp_bias_kernel(tc, xT, w1, w2_words, w2_scales, wgt, b, offs, ou
         def relu(c):
             dst = h_bf[c][:].rearrange("p (n t) -> p n t", t=PACK)
             src = h_acc[c][:].rearrange("p (t n) -> p n t", t=PACK)
-            if c in VECTOR_RELU_CHUNK:
+            if c in VECTOR_RELU_CHUNKS:
                 nc.vector.tensor_scalar_max(dst, src, 0.0)
             else:
                 nc.scalar.activation(out=dst, in_=src, func=RELU)
@@ -177,9 +168,9 @@ def tile_list_hmlp_bias_kernel(tc, xT, w1, w2_words, w2_scales, wgt, b, offs, ou
         nc.vector.transpose(wgt_turned[:], wgt_runs[:])
         repeated = wgt_repeated[:].rearrange("p (c h u) -> p c h u", h=2, u=LIST_ROWS)
         turned = wgt_turned[:].rearrange("p (h c) -> p c h", h=2).unsqueeze(3)
-        halves = [slice(half * S // 2, (half + 1) * S // 2) for half in range(2)]
-        for half in range(2):
-            runs = slice(half * LIST_ROWS // 2, (half + 1) * LIST_ROWS // 2)
+        halves = (slice(0, S // 2), slice(S // 2, S))
+        for first in (0, LIST_ROWS // 2):
+            runs = slice(first, first + LIST_ROWS // 2)
             nc.vector.tensor_copy(
                 out=repeated[:, runs], in_=turned[:, runs].to_broadcast([P, LIST_ROWS // 2, 2, LIST_ROWS])
             )
@@ -203,11 +194,12 @@ def tile_list_hmlp_bias_kernel(tc, xT, w1, w2_words, w2_scales, wgt, b, offs, ou
         quantize(x_codes[0], x_scales[0], x_bf[0], 0, S)
         for c in range(CHUNKS):
             first_layer(0, c)
+
         for c in range(CHUNKS):
             last_plane(c)
         quantize_x_chunk(0)
-        for half in range(2):
-            quantize(w_codes[1], w_scales[1], w_bf[1], half * H // 2, (half + 1) * H // 2)
+        for first in (0, H // 2):
+            quantize(w_codes[1], w_scales[1], w_bf[1], first, first + H // 2)
         first_layer(1, 0)
         for c in range(1, CHUNKS):
             quantize_x_chunk(c)

@@ -25,7 +25,8 @@ LINE = 4
 BLOCK = 32
 CHUNK = 128
 CHUNKS = S // CHUNK
-SCALAR_SHARE_W = (72, 100)
+WOVEN_AHEAD = 4
+SCALAR_SHARE_W1 = (48, 104)
 VECTOR_RELU_CHUNKS = (0, 2)
 
 
@@ -33,6 +34,7 @@ def tile_list_hmlp_bias_kernel(tc, xT, w1, w2_words, w2_scales, wgt, b, offs, ou
     nc = tc.nc
     x_planes = xT.rearrange("(a p i) t -> a i p t", p=P, i=PACK)
     w_rows = w1.rearrange("(a p i) r -> a p (i r)", p=P, i=PACK)
+    w_halves = w1.rearrange("(a p i) (h r) -> a h p i r", p=P, i=PACK, h=2)
     wgt_once = wgt.rearrange("p (h j) -> (p h) j", h=2)[:: LIST_ROWS + 1]
 
     with ExitStack() as ctx:
@@ -48,15 +50,18 @@ def tile_list_hmlp_bias_kernel(tc, xT, w1, w2_words, w2_scales, wgt, b, offs, ou
         wgt_turned = sb("wgt_turned", BLOCK, F32)
         wgt_repeated = sb("wgt_repeated", S, F32)
         x_raw = [[sb(f"x_raw{a}{i}", T, F32) for i in range(PACK)] for a in range(PASSES)]
-        w_raw = [sb(f"w_raw{a}", PACK * H, F32) for a in range(PASSES)]
-        picked = [[sb(f"picked{a}{pair}", 2 * S, F32) for pair in range(2)] for a in range(PASSES)]
-        x_bf = [sb(f"x_bf{a}", PACK * S, BF16) for a in range(PASSES)]
+        w_raw0 = [sb(f"w_raw0{h}", PACK * H // 2, F32) for h in range(2)]
+        w_raw1 = sb("w_raw1", PACK * H, F32)
+        picked1 = sb("picked1", PACK * S + CHUNK, F32)
+        picked = [sb("picked0", PACK * S, F32)[:], picked1[:, : PACK * S]]
+        x_bf = [sb("x_bf0", PACK * S, BF16), sb("x_bf1", PACK * S, BF16, tag="w_raw01")]
         w_bf = [sb(f"w_bf{a}", PACK * H, BF16) for a in range(PASSES)]
-        x_codes = [sb("x_codes0", S, U32, tag="x_raw12"), sb("x_codes1", S, U32)]
+        x_codes = [sb("x_codes0", S, U32, tag="x_raw11"), sb("x_codes1", S, U32)]
         x_scales = [sb(f"x_scales{a}", S, U8) for a in range(PASSES)]
         w_codes = [sb(f"w_codes{a}", H, U32) for a in range(PASSES)]
         w_scales = [sb(f"w_scales{a}", H, U8) for a in range(PASSES)]
-        h_bf = [sb(f"h_bf{c}", PACK * CHUNK, BF16) for c in range(CHUNKS)]
+        h_bf = [picked1[:, PACK * S - CHUNK :].bitcast(BF16)]
+        h_bf.extend(sb(f"h_bf{c}", PACK * CHUNK, BF16)[:] for c in range(1, CHUNKS))
         h_codes = [sb(f"h_codes{c}", CHUNK, U32) for c in range(CHUNKS)]
         h_scales = [sb(f"h_scales{c}", CHUNK, U8) for c in range(CHUNKS)]
         w2_codes = sb("w2_codes", 2 * M, U8)
@@ -69,21 +74,23 @@ def tile_list_hmlp_bias_kernel(tc, xT, w1, w2_words, w2_scales, wgt, b, offs, ou
         def load_x(a, i):
             nc.sync.dma_start(out=x_raw[a][i][:], in_=x_planes[a, i])
 
-        def load_w(a):
-            nc.sync.dma_start(out=w_raw[a][:], in_=w_rows[a])
+        def load_w0(h):
+            nc.sync.dma_start(out=w_raw0[h][:].rearrange("p (i r) -> p i r", i=PACK), in_=w_halves[0, h])
 
         nc.vector.memset(w2_scale_tile[:].bitcast(U32), 0)
 
         nc.sync.dma_start(out=wgt_runs[:], in_=wgt_once.rearrange("e (c n) -> e c n", n=BLOCK))
         load_x(0, 0)
         nc.sync.dma_start(offsets[:], offs)
-        for i in range(1, PACK):
-            load_x(0, i)
+        load_x(0, 1)
+        load_x(0, 2)
+        load_w0(0)
+        load_x(0, 3)
         load_x(1, 0)
-        load_w(0)
         load_x(1, 1)
+        load_w0(1)
         load_x(1, 2)
-        load_w(1)
+        nc.sync.dma_start(out=w_raw1[:], in_=w_rows[1])
         load_x(1, 3)
         nc.sync.dma_start(out=w2_codes[:].bitcast(I32), in_=w2_words[0].bitcast(I32))
         for quadrant in range(4):
@@ -94,26 +101,32 @@ def tile_list_hmlp_bias_kernel(tc, xT, w1, w2_words, w2_scales, wgt, b, offs, ou
         nc.sync.dma_start(out=bias[:], in_=b.rearrange("(p o) -> p o", o=1))
 
         def gather(a, i, j0=0, j1=S):
-            base = (i % 2) * S
+            base = i * S
             nc.vector.tensor_tensor(
-                picked[a][i // 2][:, base + j0 : base + j1],
+                picked[a][:, base + j0 : base + j1],
                 x_raw[a][i][:].indirect(offsets[:, j0 // LIST_ROWS : j1 // LIST_ROWS]),
                 weights[:, j0:j1],
                 MULT,
             )
 
-        def weave_x(a, pair, j0=0, j1=S):
+        def weave_x(a, planes, j0=0, j1=S):
             lines = slice(j0 // LINE, j1 // LINE)
-            src = picked[a][pair][:].rearrange("p (e c n) -> p c e n", e=2, n=LINE)[:, lines]
-            dst = x_bf[a][:].rearrange("p (c n h e) -> p h c e n", n=LINE, h=2, e=2)[:, pair, lines]
+            src = picked[a].rearrange("p (i c n) -> p c i n", i=PACK, n=LINE)[:, lines, planes]
+            dst = x_bf[a][:].rearrange("p (c n i) -> p c i n", n=LINE, i=PACK)[:, lines, planes]
             nc.scalar.copy(out=dst, in_=src)
 
-        def weave_w(a):
-            src = w_raw[a][:].rearrange("p (i m t) -> p m i t", i=PACK, t=PACK)
-            dst = w_bf[a][:].rearrange("p (t m i) -> p m i t", t=PACK, i=PACK)
-            share = SCALAR_SHARE_W[a]
-            nc.scalar.copy(out=dst[:, :share], in_=src[:, :share])
-            nc.vector.tensor_copy(out=dst[:, share:], in_=src[:, share:])
+        def weave_w0(h):
+            src = w_raw0[h][:].rearrange("p (g e m t) -> p m g t e", g=2, e=2, t=PACK)
+            dst = w_bf[0][:].rearrange("p (t h m g e) -> p h m g t e", t=PACK, h=2, g=2, e=2)[:, h]
+            nc.scalar.copy(out=dst, in_=src)
+
+        def weave_w1(share, ts):
+            src = w_raw1[:].rearrange("p (g e m t) -> p m g t e", g=2, e=2, t=PACK)
+            dst = w_bf[1][:].rearrange("p (t m g e) -> p m g t e", t=PACK, g=2, e=2)
+            nc.scalar.copy(out=dst[:, :share, :, ts], in_=src[:, :share, :, ts])
+            src = w_raw1[:].rearrange("p (i m t) -> p m i t", i=PACK, t=PACK)
+            dst = w_bf[1][:].rearrange("p (t m i) -> p m i t", t=PACK, i=PACK)
+            nc.vector.tensor_copy(out=dst[:, share:, :, ts], in_=src[:, share:, :, ts])
 
         def quantize(codes, scales, values, c0, c1):
             nc.vector.quantize_mx(
@@ -125,7 +138,7 @@ def tile_list_hmlp_bias_kernel(tc, xT, w1, w2_words, w2_scales, wgt, b, offs, ou
 
         def last_plane(c):
             gather(1, 3, c * CHUNK, (c + 1) * CHUNK)
-            weave_x(1, 1, c * CHUNK, (c + 1) * CHUNK)
+            weave_x(1, slice(2 if c < WOVEN_AHEAD else 0, PACK), c * CHUNK, (c + 1) * CHUNK)
 
         def first_layer(a, c):
             cols = slice(c * CHUNK, (c + 1) * CHUNK)
@@ -142,7 +155,7 @@ def tile_list_hmlp_bias_kernel(tc, xT, w1, w2_words, w2_scales, wgt, b, offs, ou
                 )
 
         def relu(c):
-            dst = h_bf[c][:].rearrange("p (n t) -> p n t", t=PACK)
+            dst = h_bf[c].rearrange("p (n t) -> p n t", t=PACK)
             src = h_acc[c][:].rearrange("p (t n) -> p n t", t=PACK)
             if c in VECTOR_RELU_CHUNKS:
                 nc.vector.tensor_scalar_max(dst, src, 0.0)
@@ -180,26 +193,28 @@ def tile_list_hmlp_bias_kernel(tc, xT, w1, w2_words, w2_scales, wgt, b, offs, ou
         for half in halves:
             gather(0, 0, half.start, half.stop)
         gather(0, 1)
-        weave_x(0, 0)
+        weave_x(0, slice(0, 2))
         gather(0, 2)
         gather(0, 3)
-        weave_x(0, 1)
+        weave_w0(0)
+        weave_x(0, slice(2, PACK))
         gather(1, 0)
-        weave_w(0)
         gather(1, 1)
-        quantize(w_codes[0], w_scales[0], w_bf[0], 0, H)
-        weave_x(1, 0)
-        gather(1, 2)
-        weave_w(1)
         quantize(x_codes[0], x_scales[0], x_bf[0], 0, S)
+        weave_w0(1)
+        weave_x(1, slice(0, 2), 0, WOVEN_AHEAD * CHUNK)
+        gather(1, 2)
+        quantize(w_codes[0], w_scales[0], w_bf[0], 0, H)
         for c in range(CHUNKS):
             first_layer(0, c)
+        for half, share in enumerate(SCALAR_SHARE_W1):
+            weave_w1(share, slice(2 * half, 2 * half + 2))
+        quantize(w_codes[1], w_scales[1], w_bf[1], 0, H // 2)
 
         for c in range(CHUNKS):
             last_plane(c)
         quantize_x_chunk(0)
-        for first in (0, H // 2):
-            quantize(w_codes[1], w_scales[1], w_bf[1], first, first + H // 2)
+        quantize(w_codes[1], w_scales[1], w_bf[1], H // 2, H)
         first_layer(1, 0)
         for c in range(1, CHUNKS):
             quantize_x_chunk(c)

@@ -26,6 +26,7 @@ BLOCK = 32
 CHUNK = 128
 CHUNKS = S // CHUNK
 WOVEN_AHEAD = 4
+SCALAR_SHARE_W0 = 80
 SCALAR_SHARE_W1 = (48, 104)
 VECTOR_RELU_CHUNKS = (0, 2)
 
@@ -34,7 +35,6 @@ def tile_list_hmlp_bias_kernel(tc, xT, w1, w2_words, w2_scales, wgt, b, offs, ou
     nc = tc.nc
     x_planes = xT.rearrange("(a p i) t -> a i p t", p=P, i=PACK)
     w_rows = w1.rearrange("(a p i) r -> a p (i r)", p=P, i=PACK)
-    w_halves = w1.rearrange("(a p i) (h r) -> a h p i r", p=P, i=PACK, h=2)
     wgt_once = wgt.rearrange("p (h j) -> (p h) j", h=2)[:: LIST_ROWS + 1]
 
     with ExitStack() as ctx:
@@ -50,11 +50,10 @@ def tile_list_hmlp_bias_kernel(tc, xT, w1, w2_words, w2_scales, wgt, b, offs, ou
         wgt_turned = sb("wgt_turned", BLOCK, F32)
         wgt_repeated = sb("wgt_repeated", S, F32)
         x_raw = [[sb(f"x_raw{a}{i}", T, F32) for i in range(PACK)] for a in range(PASSES)]
-        w_raw0 = [sb(f"w_raw0{h}", PACK * H // 2, F32) for h in range(2)]
-        w_raw1 = sb("w_raw1", PACK * H, F32)
+        w_raw = [sb(f"w_raw{a}", PACK * H, F32) for a in range(PASSES)]
         picked1 = sb("picked1", PACK * S + CHUNK, F32)
         picked = [sb("picked0", PACK * S, F32)[:], picked1[:, : PACK * S]]
-        x_bf = [sb("x_bf0", PACK * S, BF16), sb("x_bf1", PACK * S, BF16, tag="w_raw01")]
+        x_bf = [sb("x_bf0", PACK * S, BF16), sb("x_bf1", PACK * S, BF16, tag="w_raw0")]
         w_bf = [sb(f"w_bf{a}", PACK * H, BF16) for a in range(PASSES)]
         x_codes = [sb("x_codes0", S, U32, tag="x_raw11"), sb("x_codes1", S, U32)]
         x_scales = [sb(f"x_scales{a}", S, U8) for a in range(PASSES)]
@@ -74,8 +73,8 @@ def tile_list_hmlp_bias_kernel(tc, xT, w1, w2_words, w2_scales, wgt, b, offs, ou
         def load_x(a, i):
             nc.sync.dma_start(out=x_raw[a][i][:], in_=x_planes[a, i])
 
-        def load_w0(h):
-            nc.sync.dma_start(out=w_raw0[h][:].rearrange("p (i r) -> p i r", i=PACK), in_=w_halves[0, h])
+        def load_w(a):
+            nc.sync.dma_start(out=w_raw[a][:], in_=w_rows[a])
 
         nc.vector.memset(w2_scale_tile[:].bitcast(U32), 0)
 
@@ -84,13 +83,12 @@ def tile_list_hmlp_bias_kernel(tc, xT, w1, w2_words, w2_scales, wgt, b, offs, ou
         nc.sync.dma_start(offsets[:], offs)
         load_x(0, 1)
         load_x(0, 2)
-        load_w0(0)
         load_x(0, 3)
         load_x(1, 0)
         load_x(1, 1)
-        load_w0(1)
+        load_w(0)
         load_x(1, 2)
-        nc.sync.dma_start(out=w_raw1[:], in_=w_rows[1])
+        load_w(1)
         load_x(1, 3)
         nc.sync.dma_start(out=w2_codes[:].bitcast(I32), in_=w2_words[0].bitcast(I32))
         for quadrant in range(4):
@@ -115,17 +113,12 @@ def tile_list_hmlp_bias_kernel(tc, xT, w1, w2_words, w2_scales, wgt, b, offs, ou
             dst = x_bf[a][:].rearrange("p (c n i) -> p c i n", n=LINE, i=PACK)[:, lines, planes]
             nc.scalar.copy(out=dst, in_=src)
 
-        def weave_w0(h):
-            src = w_raw0[h][:].rearrange("p (g e m t) -> p m g t e", g=2, e=2, t=PACK)
-            dst = w_bf[0][:].rearrange("p (t h m g e) -> p h m g t e", t=PACK, h=2, g=2, e=2)[:, h]
-            nc.scalar.copy(out=dst, in_=src)
-
-        def weave_w1(share, ts):
-            src = w_raw1[:].rearrange("p (g e m t) -> p m g t e", g=2, e=2, t=PACK)
-            dst = w_bf[1][:].rearrange("p (t m g e) -> p m g t e", t=PACK, g=2, e=2)
+        def weave_w(a, share, ts):
+            src = w_raw[a][:].rearrange("p (g e m t) -> p m g t e", g=2, e=2, t=PACK)
+            dst = w_bf[a][:].rearrange("p (t m g e) -> p m g t e", t=PACK, g=2, e=2)
             nc.scalar.copy(out=dst[:, :share, :, ts], in_=src[:, :share, :, ts])
-            src = w_raw1[:].rearrange("p (i m t) -> p m i t", i=PACK, t=PACK)
-            dst = w_bf[1][:].rearrange("p (t m i) -> p m i t", t=PACK, i=PACK)
+            src = w_raw[a][:].rearrange("p (i m t) -> p m i t", i=PACK, t=PACK)
+            dst = w_bf[a][:].rearrange("p (t m i) -> p m i t", t=PACK, i=PACK)
             nc.vector.tensor_copy(out=dst[:, share:, :, ts], in_=src[:, share:, :, ts])
 
         def quantize(codes, scales, values, c0, c1):
@@ -196,19 +189,18 @@ def tile_list_hmlp_bias_kernel(tc, xT, w1, w2_words, w2_scales, wgt, b, offs, ou
         weave_x(0, slice(0, 2))
         gather(0, 2)
         gather(0, 3)
-        weave_w0(0)
         weave_x(0, slice(2, PACK))
         gather(1, 0)
         gather(1, 1)
         quantize(x_codes[0], x_scales[0], x_bf[0], 0, S)
-        weave_w0(1)
+        weave_w(0, SCALAR_SHARE_W0, slice(None))
         weave_x(1, slice(0, 2), 0, WOVEN_AHEAD * CHUNK)
         gather(1, 2)
         quantize(w_codes[0], w_scales[0], w_bf[0], 0, H)
         for c in range(CHUNKS):
             first_layer(0, c)
         for half, share in enumerate(SCALAR_SHARE_W1):
-            weave_w1(share, slice(2 * half, 2 * half + 2))
+            weave_w(1, share, slice(2 * half, 2 * half + 2))
         quantize(w_codes[1], w_scales[1], w_bf[1], 0, H // 2)
 
         for c in range(CHUNKS):

@@ -25,9 +25,8 @@ LINE = 4
 BLOCK = 32
 CHUNK = 128
 CHUNKS = S // CHUNK
-WOVEN_AHEAD = 4
 SCALAR_SHARE_W0 = 80
-SCALAR_SHARE_W1 = (48, 104)
+SCALAR_SHARE_W1 = (48, 88)
 VECTOR_RELU_CHUNKS = (0, 2)
 
 
@@ -51,15 +50,20 @@ def tile_list_hmlp_bias_kernel(tc, xT, w1, w2_words, w2_scales, wgt, b, offs, ou
         wgt_repeated = sb("wgt_repeated", S, F32)
         x_raw = [[sb(f"x_raw{a}{i}", T, F32) for i in range(PACK)] for a in range(PASSES)]
         w_raw = [sb(f"w_raw{a}", PACK * H, F32) for a in range(PASSES)]
-        picked1 = sb("picked1", PACK * S + CHUNK, F32)
-        picked = [sb("picked0", PACK * S, F32)[:], picked1[:, : PACK * S]]
+        picked = [[sb(f"picked{a}{pair}", 2 * S, F32) for pair in range(2 - a)] for a in range(PASSES)]
+        picked_first = sb("picked_first", 2 * CHUNK, F32)
+        picked_rest = sb("picked_rest", 2 * (S - CHUNK) + CHUNK, F32)
         x_bf = [sb("x_bf0", PACK * S, BF16), sb("x_bf1", PACK * S, BF16, tag="w_raw0")]
         w_bf = [sb(f"w_bf{a}", PACK * H, BF16) for a in range(PASSES)]
         x_codes = [sb("x_codes0", S, U32, tag="x_raw11"), sb("x_codes1", S, U32)]
         x_scales = [sb(f"x_scales{a}", S, U8) for a in range(PASSES)]
-        w_codes = [sb(f"w_codes{a}", H, U32) for a in range(PASSES)]
+        w_codes0 = sb("w_codes0", H, U32)
+        w_codes = [
+            [w_codes0[:, : H // 2], w_codes0[:, H // 2 :]],
+            [sb("w_codes10", H // 2, U32)[:], sb("w_codes11", H // 2, U32, tag="picked_first")[:]],
+        ]
         w_scales = [sb(f"w_scales{a}", H, U8) for a in range(PASSES)]
-        h_bf = [picked1[:, PACK * S - CHUNK :].bitcast(BF16)]
+        h_bf = [picked_rest[:, 2 * (S - CHUNK) - CHUNK :].bitcast(BF16)]
         h_bf.extend(sb(f"h_bf{c}", PACK * CHUNK, BF16)[:] for c in range(1, CHUNKS))
         h_codes = [sb(f"h_codes{c}", CHUNK, U32) for c in range(CHUNKS)]
         h_scales = [sb(f"h_scales{c}", CHUNK, U8) for c in range(CHUNKS)]
@@ -98,19 +102,26 @@ def tile_list_hmlp_bias_kernel(tc, xT, w1, w2_words, w2_scales, wgt, b, offs, ou
             )
         nc.sync.dma_start(out=bias[:], in_=b.rearrange("(p o) -> p o", o=1))
 
+        def picks(a, pair, j0, j1):
+            if (a, pair) != (1, 1):
+                tile, first = picked[a][pair][:], 0
+            elif j1 <= CHUNK:
+                tile, first = picked_first[:], 0
+            else:
+                tile, first = picked_rest[:, : 2 * (S - CHUNK)], CHUNK
+            return tile.rearrange("p (e j) -> p e j", e=2)[:, :, j0 - first : j1 - first]
+
         def gather(a, i, j0=0, j1=S):
-            base = i * S
             nc.vector.tensor_tensor(
-                picked[a][:, base + j0 : base + j1],
+                picks(a, i // 2, j0, j1)[:, i % 2],
                 x_raw[a][i][:].indirect(offsets[:, j0 // LIST_ROWS : j1 // LIST_ROWS]),
                 weights[:, j0:j1],
                 MULT,
             )
 
-        def weave_x(a, planes, j0=0, j1=S):
-            lines = slice(j0 // LINE, j1 // LINE)
-            src = picked[a].rearrange("p (i c n) -> p c i n", i=PACK, n=LINE)[:, lines, planes]
-            dst = x_bf[a][:].rearrange("p (c n i) -> p c i n", n=LINE, i=PACK)[:, lines, planes]
+        def weave_x(a, pair, j0=0, j1=S):
+            src = picks(a, pair, j0, j1).rearrange("p e (c n) -> p c e n", n=LINE)
+            dst = x_bf[a][:, PACK * j0 : PACK * j1].rearrange("p (c n h e) -> p h c e n", n=LINE, h=2, e=2)[:, pair]
             nc.scalar.copy(out=dst, in_=src)
 
         def weave_w(a, share, ts):
@@ -131,7 +142,7 @@ def tile_list_hmlp_bias_kernel(tc, xT, w1, w2_words, w2_scales, wgt, b, offs, ou
 
         def last_plane(c):
             gather(1, 3, c * CHUNK, (c + 1) * CHUNK)
-            weave_x(1, slice(2 if c < WOVEN_AHEAD else 0, PACK), c * CHUNK, (c + 1) * CHUNK)
+            weave_x(1, 1, c * CHUNK, (c + 1) * CHUNK)
 
         def first_layer(a, c):
             cols = slice(c * CHUNK, (c + 1) * CHUNK)
@@ -139,7 +150,7 @@ def tile_list_hmlp_bias_kernel(tc, xT, w1, w2_words, w2_scales, wgt, b, offs, ou
                 rows = slice(t * P, (t + 1) * P)
                 nc.tensor.matmul_mx(
                     out=h_acc[c][:, t * CHUNK : (t + 1) * CHUNK],
-                    lhsT=w_codes[a][:, rows].bitcast(FP8X4),
+                    lhsT=w_codes[a][t // 2][:, t % 2 * P : (t % 2 + 1) * P].bitcast(FP8X4),
                     lhsT_scale=w_scales[a][:, rows],
                     rhs=x_codes[a][:, cols].bitcast(FP8X4),
                     rhs_scale=x_scales[a][:, cols],
@@ -186,27 +197,28 @@ def tile_list_hmlp_bias_kernel(tc, xT, w1, w2_words, w2_scales, wgt, b, offs, ou
         for half in halves:
             gather(0, 0, half.start, half.stop)
         gather(0, 1)
-        weave_x(0, slice(0, 2))
+        weave_x(0, 0)
         gather(0, 2)
         gather(0, 3)
-        weave_x(0, slice(2, PACK))
+        weave_x(0, 1)
         gather(1, 0)
         gather(1, 1)
         quantize(x_codes[0], x_scales[0], x_bf[0], 0, S)
         weave_w(0, SCALAR_SHARE_W0, slice(None))
-        weave_x(1, slice(0, 2), 0, WOVEN_AHEAD * CHUNK)
-        gather(1, 2)
-        quantize(w_codes[0], w_scales[0], w_bf[0], 0, H)
+        weave_x(1, 0)
+        gather(1, 2, 0, CHUNK)
+        gather(1, 2, CHUNK, S)
+        quantize(w_codes0, w_scales[0], w_bf[0], 0, H)
         for c in range(CHUNKS):
             first_layer(0, c)
         for half, share in enumerate(SCALAR_SHARE_W1):
             weave_w(1, share, slice(2 * half, 2 * half + 2))
-        quantize(w_codes[1], w_scales[1], w_bf[1], 0, H // 2)
+        quantize(w_codes[1][0], w_scales[1], w_bf[1], 0, H // 2)
 
         for c in range(CHUNKS):
             last_plane(c)
         quantize_x_chunk(0)
-        quantize(w_codes[1], w_scales[1], w_bf[1], H // 2, H)
+        quantize(w_codes[1][1], w_scales[1][:, H // 2 :], w_bf[1][:, PACK * H // 2 :], 0, H // 2)
         first_layer(1, 0)
         for c in range(1, CHUNKS):
             quantize_x_chunk(c)

@@ -25,8 +25,7 @@ LINE = 4
 BLOCK = 32
 CHUNK = 128
 CHUNKS = S // CHUNK
-SCALAR_SHARE_W0 = 80
-SCALAR_SHARE_W1 = (48, 88)
+SCALAR_SHARE = ((44, 80), (44, 44))
 VECTOR_RELU_CHUNKS = (0, 2)
 
 
@@ -50,21 +49,25 @@ def tile_list_hmlp_bias_kernel(tc, xT, w1, w2_words, w2_scales, wgt, b, offs, ou
         wgt_repeated = sb("wgt_repeated", S, F32)
         x_raw = [[sb(f"x_raw{a}{i}", T, F32) for i in range(PACK)] for a in range(PASSES)]
         w_raw = [sb(f"w_raw{a}", PACK * H, F32) for a in range(PASSES)]
-        picked = [[sb(f"picked{a}{pair}", 2 * S, F32) for pair in range(2 - a)] for a in range(PASSES)]
-        picked_first = sb("picked_first", 2 * CHUNK, F32)
-        picked_rest = sb("picked_rest", 2 * (S - CHUNK) + CHUNK, F32)
-        x_bf = [sb("x_bf0", PACK * S, BF16), sb("x_bf1", PACK * S, BF16, tag="w_raw0")]
-        w_bf = [sb(f"w_bf{a}", PACK * H, BF16) for a in range(PASSES)]
-        x_codes = [sb("x_codes0", S, U32, tag="x_raw11"), sb("x_codes1", S, U32)]
+        picked = [[sb(f"picked{a}{pair}", 2 * S, F32) for pair in range(2)] for a in range(PASSES)]
+        x_bf = [sb(f"x_bf{a}", PACK * S, BF16) for a in range(PASSES)]
+        w_bf = [[sb(f"w_bf{a}{half}", PACK * H // 2, BF16) for half in range(2)] for a in range(PASSES)]
+        x_codes0 = sb("x_codes0", S, U32, tag="x_raw11")
+        x_early = sb("x_early", S // 2, U32)
+        x_late = sb("x_late", S // 2, U32, tag="w_raw1")
+
+        def x_codes(a, j0, j1):
+            if a == 0:
+                return x_codes0[:, j0:j1]
+            return x_early[:, j0:j1] if j1 <= S // 2 else x_late[:, j0 - S // 2 : j1 - S // 2]
+
         x_scales = [sb(f"x_scales{a}", S, U8) for a in range(PASSES)]
-        w_codes0 = sb("w_codes0", H, U32)
         w_codes = [
-            [w_codes0[:, : H // 2], w_codes0[:, H // 2 :]],
-            [sb("w_codes10", H // 2, U32)[:], sb("w_codes11", H // 2, U32, tag="picked_first")[:]],
+            [sb("w_codes00", H // 2, U32)[:], sb("w_codes01", H // 2, U32)[:]],
+            [sb("w_codes10", H // 2, U32)[:], sb("w_codes11", H // 2, U32)[:]],
         ]
         w_scales = [sb(f"w_scales{a}", H, U8) for a in range(PASSES)]
-        h_bf = [picked_rest[:, 2 * (S - CHUNK) - CHUNK :].bitcast(BF16)]
-        h_bf.extend(sb(f"h_bf{c}", PACK * CHUNK, BF16)[:] for c in range(1, CHUNKS))
+        h_bf = [sb(f"h_bf{c}", PACK * CHUNK, BF16) for c in range(CHUNKS)]
         h_codes = [sb(f"h_codes{c}", CHUNK, U32) for c in range(CHUNKS)]
         h_scales = [sb(f"h_scales{c}", CHUNK, U8) for c in range(CHUNKS)]
         w2_codes = sb("w2_codes", 2 * M, U8)
@@ -85,15 +88,11 @@ def tile_list_hmlp_bias_kernel(tc, xT, w1, w2_words, w2_scales, wgt, b, offs, ou
         nc.sync.dma_start(out=wgt_runs[:], in_=wgt_once.rearrange("e (c n) -> e c n", n=BLOCK))
         load_x(0, 0)
         nc.sync.dma_start(offsets[:], offs)
-        load_x(0, 1)
-        load_x(0, 2)
-        load_x(0, 3)
-        load_x(1, 0)
-        load_x(1, 1)
+        for plane in range(1, PASSES * PACK - 1):
+            load_x(*divmod(plane, PACK))
         load_w(0)
-        load_x(1, 2)
-        load_w(1)
         load_x(1, 3)
+        load_w(1)
         nc.sync.dma_start(out=w2_codes[:].bitcast(I32), in_=w2_words[0].bitcast(I32))
         for quadrant in range(4):
             nc.sync.dma_start(
@@ -103,13 +102,7 @@ def tile_list_hmlp_bias_kernel(tc, xT, w1, w2_words, w2_scales, wgt, b, offs, ou
         nc.sync.dma_start(out=bias[:], in_=b.rearrange("(p o) -> p o", o=1))
 
         def picks(a, pair, j0, j1):
-            if (a, pair) != (1, 1):
-                tile, first = picked[a][pair][:], 0
-            elif j1 <= CHUNK:
-                tile, first = picked_first[:], 0
-            else:
-                tile, first = picked_rest[:, : 2 * (S - CHUNK)], CHUNK
-            return tile.rearrange("p (e j) -> p e j", e=2)[:, :, j0 - first : j1 - first]
+            return picked[a][pair][:].rearrange("p (e j) -> p e j", e=2)[:, :, j0:j1]
 
         def gather(a, i, j0=0, j1=S):
             nc.vector.tensor_tensor(
@@ -119,47 +112,49 @@ def tile_list_hmlp_bias_kernel(tc, xT, w1, w2_words, w2_scales, wgt, b, offs, ou
                 MULT,
             )
 
-        def weave_x(a, pair, j0=0, j1=S):
+        def weave_x(copy, a, pair, j0=0, j1=S):
             src = picks(a, pair, j0, j1).rearrange("p e (c n) -> p c e n", n=LINE)
             dst = x_bf[a][:, PACK * j0 : PACK * j1].rearrange("p (c n h e) -> p h c e n", n=LINE, h=2, e=2)[:, pair]
-            nc.scalar.copy(out=dst, in_=src)
+            copy(out=dst, in_=src)
 
-        def weave_w(a, share, ts):
+        def weave_w_scalar(a, half):
+            share = SCALAR_SHARE[a][half]
             src = w_raw[a][:].rearrange("p (g e m t) -> p m g t e", g=2, e=2, t=PACK)
-            dst = w_bf[a][:].rearrange("p (t m g e) -> p m g t e", t=PACK, g=2, e=2)
-            nc.scalar.copy(out=dst[:, :share, :, ts], in_=src[:, :share, :, ts])
-            src = w_raw[a][:].rearrange("p (i m t) -> p m i t", i=PACK, t=PACK)
-            dst = w_bf[a][:].rearrange("p (t m i) -> p m i t", t=PACK, i=PACK)
-            nc.vector.tensor_copy(out=dst[:, share:, :, ts], in_=src[:, share:, :, ts])
+            dst = w_bf[a][half][:].rearrange("p (t m g e) -> p m g t e", t=2, g=2, e=2)
+            nc.scalar.copy(out=dst[:, :share], in_=src[:, :share, :, 2 * half : 2 * half + 2])
 
-        def quantize(codes, scales, values, c0, c1):
-            nc.vector.quantize_mx(
-                out=codes[:, c0:c1].bitcast(FP8X4), scales=scales[:, c0:c1], in_=values[:, PACK * c0 : PACK * c1]
+        def weave_w_vector(a, half):
+            share = SCALAR_SHARE[a][half]
+            src = w_raw[a][:].rearrange("p (i m t) -> p m i t", i=PACK, t=PACK)
+            dst = w_bf[a][half][:].rearrange("p (t m i) -> p m i t", t=2, i=PACK)
+            nc.vector.tensor_copy(out=dst[:, share:], in_=src[:, share:, :, 2 * half : 2 * half + 2])
+
+        def quantize(codes, scales, values):
+            nc.vector.quantize_mx(out=codes.bitcast(FP8X4), scales=scales, in_=values)
+
+        def quantize_x(a, j0, j1):
+            quantize(x_codes(a, j0, j1), x_scales[a][:, j0:j1], x_bf[a][:, PACK * j0 : PACK * j1])
+
+        def quantize_w(a, t0, t1):
+            half, c0, c1 = t0 // 2, t0 % 2 * P, (t1 - t0 // 2 * 2) * P
+            quantize(
+                w_codes[a][half][:, c0:c1], w_scales[a][:, t0 * P : t1 * P], w_bf[a][half][:, PACK * c0 : PACK * c1]
             )
 
-        def quantize_x_chunk(c):
-            quantize(x_codes[1], x_scales[1], x_bf[1], c * CHUNK, (c + 1) * CHUNK)
-
-        def last_plane(c):
-            gather(1, 3, c * CHUNK, (c + 1) * CHUNK)
-            weave_x(1, 1, c * CHUNK, (c + 1) * CHUNK)
-
-        def first_layer(a, c):
+        def first_layer(a, c, t):
             cols = slice(c * CHUNK, (c + 1) * CHUNK)
-            for t in range(PACK):
-                rows = slice(t * P, (t + 1) * P)
-                nc.tensor.matmul_mx(
-                    out=h_acc[c][:, t * CHUNK : (t + 1) * CHUNK],
-                    lhsT=w_codes[a][t // 2][:, t % 2 * P : (t % 2 + 1) * P].bitcast(FP8X4),
-                    lhsT_scale=w_scales[a][:, rows],
-                    rhs=x_codes[a][:, cols].bitcast(FP8X4),
-                    rhs_scale=x_scales[a][:, cols],
-                    start=(a == 0 and t == 0),
-                    stop=(a == PASSES - 1 and t == PACK - 1),
-                )
+            nc.tensor.matmul_mx(
+                out=h_acc[c][:, t * CHUNK : (t + 1) * CHUNK],
+                lhsT=w_codes[a][t // 2][:, t % 2 * P : (t % 2 + 1) * P].bitcast(FP8X4),
+                lhsT_scale=w_scales[a][:, t * P : (t + 1) * P],
+                rhs=x_codes(a, cols.start, cols.stop).bitcast(FP8X4),
+                rhs_scale=x_scales[a][:, cols],
+                start=(a == 0 and t == 0),
+                stop=(a == PASSES - 1 and t == PACK - 1),
+            )
 
         def relu(c):
-            dst = h_bf[c].rearrange("p (n t) -> p n t", t=PACK)
+            dst = h_bf[c][:].rearrange("p (n t) -> p n t", t=PACK)
             src = h_acc[c][:].rearrange("p (t n) -> p n t", t=PACK)
             if c in VECTOR_RELU_CHUNKS:
                 nc.vector.tensor_scalar_max(dst, src, 0.0)
@@ -167,7 +162,7 @@ def tile_list_hmlp_bias_kernel(tc, xT, w1, w2_words, w2_scales, wgt, b, offs, ou
                 nc.scalar.activation(out=dst, in_=src, func=RELU)
 
         def second_layer(c):
-            quantize(h_codes[c], h_scales[c], h_bf[c], 0, CHUNK)
+            quantize(h_codes[c][:], h_scales[c][:], h_bf[c][:])
             nc.tensor.matmul_mx(
                 out=y_acc[c][:],
                 lhsT=w2_codes[:].bitcast(FP4X4),
@@ -197,32 +192,40 @@ def tile_list_hmlp_bias_kernel(tc, xT, w1, w2_words, w2_scales, wgt, b, offs, ou
         for half in halves:
             gather(0, 0, half.start, half.stop)
         gather(0, 1)
-        weave_x(0, 0)
+        weave_x(nc.scalar.copy, 0, 0)
         gather(0, 2)
         gather(0, 3)
-        weave_x(0, 1)
+        weave_x(nc.scalar.copy, 0, 1)
         gather(1, 0)
         gather(1, 1)
-        quantize(x_codes[0], x_scales[0], x_bf[0], 0, S)
-        weave_w(0, SCALAR_SHARE_W0, slice(None))
-        weave_x(1, 0)
-        gather(1, 2, 0, CHUNK)
-        gather(1, 2, CHUNK, S)
-        quantize(w_codes0, w_scales[0], w_bf[0], 0, H)
+        weave_x(nc.scalar.copy, 1, 0)
+        gather(1, 2)
+        quantize_x(0, 0, S)
+        for half in range(2):
+            weave_w_scalar(0, half)
+            weave_w_vector(0, half)
+        quantize_w(0, 0, 2)
         for c in range(CHUNKS):
-            first_layer(0, c)
-        for half, share in enumerate(SCALAR_SHARE_W1):
-            weave_w(1, share, slice(2 * half, 2 * half + 2))
-        quantize(w_codes[1][0], w_scales[1], w_bf[1], 0, H // 2)
+            gather(1, 3, c * CHUNK, (c + 1) * CHUNK)
+        for c in range(CHUNKS - 1):
+            weave_x(nc.scalar.copy, 1, 1, c * CHUNK, (c + 1) * CHUNK)
+        quantize_w(0, 2, 4)
+        for t in range(PACK):
+            for c in range(CHUNKS):
+                first_layer(0, c, t)
+        weave_x(nc.vector.tensor_copy, 1, 1, S - CHUNK, S)
+        quantize_x(1, 0, 2 * CHUNK)
 
+        for half in range(2):
+            weave_w_scalar(1, half)
+            weave_w_vector(1, half)
+        for t in range(PACK):
+            quantize_w(1, t, t + 1)
+        for c in range(CHUNKS // 2, CHUNKS):
+            quantize_x(1, c * CHUNK, (c + 1) * CHUNK)
         for c in range(CHUNKS):
-            last_plane(c)
-        quantize_x_chunk(0)
-        quantize(w_codes[1][1], w_scales[1][:, H // 2 :], w_bf[1][:, PACK * H // 2 :], 0, H // 2)
-        first_layer(1, 0)
-        for c in range(1, CHUNKS):
-            quantize_x_chunk(c)
-            first_layer(1, c)
+            for t in range(PACK):
+                first_layer(1, c, t)
         for c in range(CHUNKS):
             relu(c)
         for c in range(CHUNKS):

@@ -25,7 +25,7 @@ LINE = 4
 BLOCK = 32
 CHUNK = 128
 CHUNKS = S // CHUNK
-SCALAR_SHARE = ((44, 80), (44, 44))
+SCALAR_SHARE = ((28, 92), (44, 44))
 VECTOR_RELU_CHUNKS = (0, 2)
 
 
@@ -49,10 +49,13 @@ def tile_list_hmlp_bias_kernel(tc, xT, w1, w2_words, w2_scales, wgt, b, offs, ou
         wgt_repeated = sb("wgt_repeated", S, F32)
         x_raw = [[sb(f"x_raw{a}{i}", T, F32) for i in range(PACK)] for a in range(PASSES)]
         w_raw = [sb(f"w_raw{a}", PACK * H, F32) for a in range(PASSES)]
-        picked = [[sb(f"picked{a}{pair}", 2 * S, F32) for pair in range(2)] for a in range(PASSES)]
+        picked = [[sb(f"picked{a}{pair}", 2 * S, F32) for pair in range(2 - a)] for a in range(PASSES)]
+        picked_first = sb("picked_first", 2 * CHUNK, F32)
+        picked_rest = sb("picked_rest", 2 * (S - CHUNK), F32)
         x_bf = [sb(f"x_bf{a}", PACK * S, BF16) for a in range(PASSES)]
         w_bf = [[sb(f"w_bf{a}{half}", PACK * H // 2, BF16) for half in range(2)] for a in range(PASSES)]
-        x_codes0 = sb("x_codes0", S, U32, tag="x_raw11")
+        weights_again = sb("weights_again", S, F32)
+        x_codes0 = sb("x_codes0", S, U32, tag="weights_again")
         x_early = sb("x_early", S // 2, U32)
         x_late = sb("x_late", S // 2, U32, tag="w_raw1")
 
@@ -63,7 +66,7 @@ def tile_list_hmlp_bias_kernel(tc, xT, w1, w2_words, w2_scales, wgt, b, offs, ou
 
         x_scales = [sb(f"x_scales{a}", S, U8) for a in range(PASSES)]
         w_codes = [
-            [sb("w_codes00", H // 2, U32)[:], sb("w_codes01", H // 2, U32)[:]],
+            [sb("w_codes00", H // 2, U32)[:], sb("w_codes01", H // 2, U32, tag="picked_first")[:]],
             [sb("w_codes10", H // 2, U32)[:], sb("w_codes11", H // 2, U32)[:]],
         ]
         w_scales = [sb(f"w_scales{a}", H, U8) for a in range(PASSES)]
@@ -102,13 +105,19 @@ def tile_list_hmlp_bias_kernel(tc, xT, w1, w2_words, w2_scales, wgt, b, offs, ou
         nc.sync.dma_start(out=bias[:], in_=b.rearrange("(p o) -> p o", o=1))
 
         def picks(a, pair, j0, j1):
-            return picked[a][pair][:].rearrange("p (e j) -> p e j", e=2)[:, :, j0:j1]
+            if (a, pair) != (1, 1):
+                tile, first = picked[a][pair], 0
+            elif j1 <= CHUNK:
+                tile, first = picked_first, 0
+            else:
+                tile, first = picked_rest, CHUNK
+            return tile[:].rearrange("p (e j) -> p e j", e=2)[:, :, j0 - first : j1 - first]
 
-        def gather(a, i, j0=0, j1=S):
+        def gather(a, i, j0=0, j1=S, factors=weights):
             nc.vector.tensor_tensor(
                 picks(a, i // 2, j0, j1)[:, i % 2],
                 x_raw[a][i][:].indirect(offsets[:, j0 // LIST_ROWS : j1 // LIST_ROWS]),
-                weights[:, j0:j1],
+                factors[:, j0:j1],
                 MULT,
             )
 
@@ -197,9 +206,13 @@ def tile_list_hmlp_bias_kernel(tc, xT, w1, w2_words, w2_scales, wgt, b, offs, ou
         gather(0, 3)
         weave_x(nc.scalar.copy, 0, 1)
         gather(1, 0)
-        gather(1, 1)
-        weave_x(nc.scalar.copy, 1, 0)
-        gather(1, 2)
+        nc.scalar.copy(out=weights_again[:, : S - CHUNK], in_=weights[:, : S - CHUNK])
+        gather(1, 1, 0, S - CHUNK, weights_again)
+        weave_x(nc.scalar.copy, 1, 0, 0, S - CHUNK)
+        gather(1, 1, S - CHUNK, S)
+        weave_x(nc.scalar.copy, 1, 0, S - CHUNK, S)
+        gather(1, 2, 0, CHUNK)
+        gather(1, 2, CHUNK, S)
         quantize_x(0, 0, S)
         for half in range(2):
             weave_w_scalar(0, half)
@@ -207,13 +220,13 @@ def tile_list_hmlp_bias_kernel(tc, xT, w1, w2_words, w2_scales, wgt, b, offs, ou
         quantize_w(0, 0, 2)
         for c in range(CHUNKS):
             gather(1, 3, c * CHUNK, (c + 1) * CHUNK)
-        for c in range(CHUNKS - 1):
+        for c in (0, 1, 3):
             weave_x(nc.scalar.copy, 1, 1, c * CHUNK, (c + 1) * CHUNK)
+        weave_x(nc.vector.tensor_copy, 1, 1, 2 * CHUNK, 3 * CHUNK)
         quantize_w(0, 2, 4)
         for t in range(PACK):
             for c in range(CHUNKS):
                 first_layer(0, c, t)
-        weave_x(nc.vector.tensor_copy, 1, 1, S - CHUNK, S)
         quantize_x(1, 0, 2 * CHUNK)
 
         for half in range(2):

@@ -25,7 +25,7 @@ LINE = 4
 BLOCK = 32
 CHUNK = 128
 CHUNKS = S // CHUNK
-SCALAR_SHARE = ((28, 92), (44, 44))
+SCALAR_SHARE = ((52, 92), (44, 44))
 VECTOR_RELU_CHUNKS = (0, 2)
 
 
@@ -49,9 +49,8 @@ def tile_list_hmlp_bias_kernel(tc, xT, w1, w2_words, w2_scales, wgt, b, offs, ou
         wgt_repeated = sb("wgt_repeated", S, F32)
         x_raw = [[sb(f"x_raw{a}{i}", T, F32) for i in range(PACK)] for a in range(PASSES)]
         w_raw = [sb(f"w_raw{a}", PACK * H, F32) for a in range(PASSES)]
-        picked = [[sb(f"picked{a}{pair}", 2 * S, F32) for pair in range(2 - a)] for a in range(PASSES)]
-        picked_first = sb("picked_first", 2 * CHUNK, F32)
-        picked_rest = sb("picked_rest", 2 * (S - CHUNK), F32)
+        picked = [[sb(f"picked{a}{pair}", 2 * S, F32) for pair in range(2)] for a in range(PASSES)]
+        weights_third = sb("weights_third", 2 * CHUNK, F32)
         x_bf = [sb(f"x_bf{a}", PACK * S, BF16) for a in range(PASSES)]
         w_bf = [[sb(f"w_bf{a}{half}", PACK * H // 2, BF16) for half in range(2)] for a in range(PASSES)]
         weights_again = sb("weights_again", S, F32)
@@ -66,7 +65,7 @@ def tile_list_hmlp_bias_kernel(tc, xT, w1, w2_words, w2_scales, wgt, b, offs, ou
 
         x_scales = [sb(f"x_scales{a}", S, U8) for a in range(PASSES)]
         w_codes = [
-            [sb("w_codes00", H // 2, U32)[:], sb("w_codes01", H // 2, U32, tag="picked_first")[:]],
+            [sb("w_codes00", H // 2, U32)[:], sb("w_codes01", H // 2, U32, tag="weights_third")[:]],
             [sb("w_codes10", H // 2, U32)[:], sb("w_codes11", H // 2, U32)[:]],
         ]
         w_scales = [sb(f"w_scales{a}", H, U8) for a in range(PASSES)]
@@ -105,13 +104,7 @@ def tile_list_hmlp_bias_kernel(tc, xT, w1, w2_words, w2_scales, wgt, b, offs, ou
         nc.sync.dma_start(out=bias[:], in_=b.rearrange("(p o) -> p o", o=1))
 
         def picks(a, pair, j0, j1):
-            if (a, pair) != (1, 1):
-                tile, first = picked[a][pair], 0
-            elif j1 <= CHUNK:
-                tile, first = picked_first, 0
-            else:
-                tile, first = picked_rest, CHUNK
-            return tile[:].rearrange("p (e j) -> p e j", e=2)[:, :, j0 - first : j1 - first]
+            return picked[a][pair][:].rearrange("p (e j) -> p e j", e=2)[:, :, j0:j1]
 
         def gather(a, i, j0=0, j1=S, factors=weights):
             nc.vector.tensor_tensor(
@@ -211,19 +204,21 @@ def tile_list_hmlp_bias_kernel(tc, xT, w1, w2_words, w2_scales, wgt, b, offs, ou
         weave_x(nc.scalar.copy, 1, 0, 0, S - CHUNK)
         gather(1, 1, S - CHUNK, S)
         weave_x(nc.scalar.copy, 1, 0, S - CHUNK, S)
-        gather(1, 2, 0, CHUNK)
-        gather(1, 2, CHUNK, S)
+        gather(1, 2)
         quantize_x(0, 0, S)
         for half in range(2):
             weave_w_scalar(0, half)
             weave_w_vector(0, half)
         quantize_w(0, 0, 2)
-        for c in range(CHUNKS):
-            gather(1, 3, c * CHUNK, (c + 1) * CHUNK)
+        nc.scalar.copy(out=weights_third[:, CHUNK:], in_=weights[:, CHUNK : 2 * CHUNK])
+        gather(1, 3, 0, CHUNK)
+        gather(1, 3, CHUNK, 2 * CHUNK, weights_third)
+        gather(1, 3, 2 * CHUNK, S)
         for c in (0, 1, 3):
             weave_x(nc.scalar.copy, 1, 1, c * CHUNK, (c + 1) * CHUNK)
-        weave_x(nc.vector.tensor_copy, 1, 1, 2 * CHUNK, 3 * CHUNK)
+
         quantize_w(0, 2, 4)
+        weave_x(nc.vector.tensor_copy, 1, 1, 2 * CHUNK, 3 * CHUNK)
         for t in range(PACK):
             for c in range(CHUNKS):
                 first_layer(0, c, t)

@@ -121,8 +121,8 @@ def tile_list_hmlp_bias_kernel(tc, xT, w1, w2_words, w2_scales, wgt, b, offs, ou
 
         def weave_w_scalar(a, half):
             share = SCALAR_SHARE[a][half]
-            src = w_raw[a][:].rearrange("p (g e m t) -> p m g t e", g=2, e=2, t=PACK)
-            dst = w_bf[a][half][:].rearrange("p (t m g e) -> p m g t e", t=2, g=2, e=2)
+            src = w_raw[a][:].rearrange("p (i m t) -> p m i t", i=PACK, t=PACK)
+            dst = w_bf[a][half][:].rearrange("p (t m i) -> p m i t", t=2, i=PACK)
             nc.scalar.copy(out=dst[:, :share], in_=src[:, :share, :, 2 * half : 2 * half + 2])
 
         def weave_w_vector(a, half):

@@ -155,9 +155,9 @@ def tile_list_hmlp_bias_kernel(tc, xT, w1, w2_words, w2_scales, wgt, b, offs, ou
                 stop=(a == PASSES - 1 and t == PACK - 1),
             )
 
-        def relu(c):
-            dst = h_bf[c][:].rearrange("p (n t) -> p n t", t=PACK)
-            src = h_acc[c][:].rearrange("p (t n) -> p n t", t=PACK)
+        def relu(c, n0=0, n1=CHUNK):
+            dst = h_bf[c][:].rearrange("p (n t) -> p n t", t=PACK)[:, n0:n1]
+            src = h_acc[c][:].rearrange("p (t n) -> p n t", t=PACK)[:, n0:n1]
             if c in VECTOR_RELU_CHUNKS:
                 nc.vector.tensor_scalar_max(dst, src, 0.0)
             else:
@@ -234,9 +234,14 @@ def tile_list_hmlp_bias_kernel(tc, xT, w1, w2_words, w2_scales, wgt, b, offs, ou
         for c in range(CHUNKS):
             for t in range(PACK):
                 first_layer(1, c, t)
-        for c in range(CHUNKS):
-            relu(c)
-        for c in range(CHUNKS):
-            second_layer(c)
-        for c in range(CHUNKS):
+        relu(0)
+        relu(1)
+        relu(2, 0, CHUNK // 2)
+        relu(3)
+        second_layer(0)
+        second_layer(1)
+        relu(2, CHUNK // 2, CHUNK)
+        second_layer(3)
+        second_layer(2)
+        for c in (0, 1, 3, 2):
             finish(c)

@@ -119,6 +119,16 @@ def tile_list_hmlp_bias_kernel(tc, xT, w1, w2_words, w2_scales, wgt, b, offs, ou
             dst = x_bf[a][:, PACK * j0 : PACK * j1].rearrange("p (c n h e) -> p h c e n", n=LINE, h=2, e=2)[:, pair]
             copy(out=dst, in_=src)
 
+        def weave_dealt(copy, a, pair, c):
+            src = picks(a, pair, c * CHUNK, (c + 1) * CHUNK).rearrange("p e (u c n) -> p u c e n", u=2, n=LINE)
+            dst = x_bf[a][:, PACK * S // 2 :].rearrange("p (u d c n h e) -> p d h u c e n", u=2, d=2, n=LINE, h=2, e=2)
+            copy(out=dst[:, c - 2, pair], in_=src)
+
+        def weave_pair(a, pair):
+            weave_x(nc.scalar.copy, a, pair, 0, S // 2)
+            for c in (2, 3):
+                weave_dealt(nc.scalar.copy, a, pair, c)
+
         def weave_w_scalar(a, half):
             share = SCALAR_SHARE[a][half]
             src = w_raw[a][:].rearrange("p (i m t) -> p m i t", i=PACK, t=PACK)
@@ -155,9 +165,14 @@ def tile_list_hmlp_bias_kernel(tc, xT, w1, w2_words, w2_scales, wgt, b, offs, ou
                 stop=(a == PASSES - 1 and t == PACK - 1),
             )
 
-        def relu(c, n0=0, n1=CHUNK):
-            dst = h_bf[c][:].rearrange("p (n t) -> p n t", t=PACK)[:, n0:n1]
-            src = h_acc[c][:].rearrange("p (t n) -> p n t", t=PACK)[:, n0:n1]
+        def relu(c, half=None):
+            src = h_acc[c][:].rearrange("p (t n) -> p n t", t=PACK)
+            if half is None:
+                dst = h_bf[c][:].rearrange("p (n t) -> p n t", t=PACK)
+            else:
+                n0 = (c - 2) * CHUNK // 2
+                dst = h_bf[2 + half][:].rearrange("p (n t) -> p n t", t=PACK)[:, n0 : n0 + CHUNK // 2]
+                src = src[:, half * CHUNK // 2 : (half + 1) * CHUNK // 2]
             if c in VECTOR_RELU_CHUNKS:
                 nc.vector.tensor_scalar_max(dst, src, 0.0)
             else:
@@ -194,16 +209,17 @@ def tile_list_hmlp_bias_kernel(tc, xT, w1, w2_words, w2_scales, wgt, b, offs, ou
         for half in halves:
             gather(0, 0, half.start, half.stop)
         gather(0, 1)
-        weave_x(nc.scalar.copy, 0, 0)
+        weave_pair(0, 0)
         gather(0, 2)
         gather(0, 3)
-        weave_x(nc.scalar.copy, 0, 1)
+        weave_pair(0, 1)
         gather(1, 0)
         nc.scalar.copy(out=weights_again[:, : S - CHUNK], in_=weights[:, : S - CHUNK])
         gather(1, 1, 0, S - CHUNK, weights_again)
-        weave_x(nc.scalar.copy, 1, 0, 0, S - CHUNK)
+        weave_x(nc.scalar.copy, 1, 0, 0, S // 2)
+        weave_dealt(nc.scalar.copy, 1, 0, 2)
         gather(1, 1, S - CHUNK, S)
-        weave_x(nc.scalar.copy, 1, 0, S - CHUNK, S)
+        weave_dealt(nc.scalar.copy, 1, 0, 3)
         gather(1, 2)
         quantize_x(0, 0, S)
         for half in range(2):
@@ -214,11 +230,12 @@ def tile_list_hmlp_bias_kernel(tc, xT, w1, w2_words, w2_scales, wgt, b, offs, ou
         gather(1, 3, 0, CHUNK)
         gather(1, 3, CHUNK, 2 * CHUNK, weights_third)
         gather(1, 3, 2 * CHUNK, S)
-        for c in (0, 1, 3):
+        for c in (0, 1):
             weave_x(nc.scalar.copy, 1, 1, c * CHUNK, (c + 1) * CHUNK)
+        weave_dealt(nc.scalar.copy, 1, 1, 3)
 
         quantize_w(0, 2, 4)
-        weave_x(nc.vector.tensor_copy, 1, 1, 2 * CHUNK, 3 * CHUNK)
+        weave_dealt(nc.vector.tensor_copy, 1, 1, 2)
         for t in range(PACK):
             for c in range(CHUNKS):
                 first_layer(0, c, t)
@@ -236,12 +253,12 @@ def tile_list_hmlp_bias_kernel(tc, xT, w1, w2_words, w2_scales, wgt, b, offs, ou
                 first_layer(1, c, t)
         relu(0)
         relu(1)
-        relu(2, 0, CHUNK // 2)
-        relu(3)
+        relu(2, 0)
+        relu(3, 0)
+        relu(3, 1)
         second_layer(0)
-        second_layer(1)
-        relu(2, CHUNK // 2, CHUNK)
-        second_layer(3)
-        second_layer(2)
-        for c in (0, 1, 3, 2):
+        relu(2, 1)
+        for c in range(1, CHUNKS):
+            second_layer(c)
+        for c in range(CHUNKS):
             finish(c)

@@ -26,7 +26,6 @@ BLOCK = 32
 CHUNK = 128
 CHUNKS = S // CHUNK
 SCALAR_SHARE = ((52, 92), (44, 44))
-VECTOR_RELU_CHUNKS = (0, 2)
 
 
 def tile_list_hmlp_bias_kernel(tc, xT, w1, w2_words, w2_scales, wgt, b, offs, out):
@@ -76,8 +75,10 @@ def tile_list_hmlp_bias_kernel(tc, xT, w1, w2_words, w2_scales, wgt, b, offs, ou
         w2_scale_tile = sb("w2_scale_tile", M, U8)
         bias = sb("bias", 1, F32)
         result = [sb(f"result{c}", CHUNK, F32) for c in range(CHUNKS)]
-        h_acc = [psum.tile([P, PACK * CHUNK], F32, name=f"h_acc{c}") for c in range(CHUNKS)]
-        y_acc = [psum.tile([P, CHUNK], F32, name=f"y_acc{c}") for c in range(CHUNKS)]
+        h_whole = {c: psum.tile([P, PACK * CHUNK], F32, name=f"h_whole{c}") for c in (0, 2, 3)}
+        h_halves = [psum.tile([P, 2 * CHUNK], F32, name=f"h_half{half}") for half in range(2)]
+        y_acc = {c: psum.tile([P, CHUNK], F32, name=f"y_acc{c}") for c in (0, 2, 3)}
+        y_acc[1] = psum.tile([P, CHUNK], F32, name="y_acc1", tag="h_half0")
 
         def load_x(a, i):
             nc.sync.dma_start(out=x_raw[a][i][:], in_=x_planes[a, i])
@@ -155,28 +156,33 @@ def tile_list_hmlp_bias_kernel(tc, xT, w1, w2_words, w2_scales, wgt, b, offs, ou
 
         def first_layer(a, c, t):
             cols = slice(c * CHUNK, (c + 1) * CHUNK)
+            bank, place, last = (h_halves[t // 2], t % 2, 1) if c == 1 else (h_whole[c], t, PACK - 1)
             nc.tensor.matmul_mx(
-                out=h_acc[c][:, t * CHUNK : (t + 1) * CHUNK],
+                out=bank[:, place * CHUNK : (place + 1) * CHUNK],
                 lhsT=w_codes[a][t // 2][:, t % 2 * P : (t % 2 + 1) * P].bitcast(FP8X4),
                 lhsT_scale=w_scales[a][:, t * P : (t + 1) * P],
                 rhs=x_codes(a, cols.start, cols.stop).bitcast(FP8X4),
                 rhs_scale=x_scales[a][:, cols],
-                start=(a == 0 and t == 0),
-                stop=(a == PASSES - 1 and t == PACK - 1),
+                start=(a == 0 and place == 0),
+                stop=(a == PASSES - 1 and place == last),
             )
 
-        def relu(c, half=None):
-            src = h_acc[c][:].rearrange("p (t n) -> p n t", t=PACK)
-            if half is None:
-                dst = h_bf[c][:].rearrange("p (n t) -> p n t", t=PACK)
-            else:
-                n0 = (c - 2) * CHUNK // 2
-                dst = h_bf[2 + half][:].rearrange("p (n t) -> p n t", t=PACK)[:, n0 : n0 + CHUNK // 2]
-                src = src[:, half * CHUNK // 2 : (half + 1) * CHUNK // 2]
-            if c in VECTOR_RELU_CHUNKS:
-                nc.vector.tensor_scalar_max(dst, src, 0.0)
-            else:
-                nc.scalar.activation(out=dst, in_=src, func=RELU)
+        def relu_vector(dst, src):
+            nc.vector.tensor_scalar_max(dst, src, 0.0)
+
+        def relu_scalar(dst, src):
+            nc.scalar.activation(out=dst, in_=src, func=RELU)
+
+        def by_token(tile, slots=PACK):
+            return tile[:].rearrange("p (t n) -> p n t", t=slots)
+
+        def rounded(c):
+            return h_bf[c][:].rearrange("p (n t) -> p n t", t=PACK)
+
+        def dealt(bank, half):
+            n0 = (bank - 2) * CHUNK // 2
+            src = by_token(h_whole[bank])[:, half * CHUNK // 2 : (half + 1) * CHUNK // 2]
+            return rounded(2 + half)[:, n0 : n0 + CHUNK // 2], src
 
         def second_layer(c):
             quantize(h_codes[c][:], h_scales[c][:], h_bf[c][:])
@@ -248,17 +254,22 @@ def tile_list_hmlp_bias_kernel(tc, xT, w1, w2_words, w2_scales, wgt, b, offs, ou
             quantize_w(1, t, t + 1)
         for c in range(CHUNKS // 2, CHUNKS):
             quantize_x(1, c * CHUNK, (c + 1) * CHUNK)
-        for c in range(CHUNKS):
+        for t in range(PACK):
+            first_layer(1, 1, t)
+            first_layer(1, 0, t)
+        for c in range(CHUNKS // 2, CHUNKS):
             for t in range(PACK):
                 first_layer(1, c, t)
-        relu(0)
-        relu(1)
-        relu(2, 0)
-        relu(3, 0)
-        relu(3, 1)
+        for half in range(2):
+            relu_scalar(rounded(1)[:, :, 2 * half : 2 * half + 2], by_token(h_halves[half], 2))
+        relu_vector(rounded(0), by_token(h_whole[0]))
+        relu_scalar(*dealt(2, 0))
+        relu_scalar(*dealt(3, 0))
+        relu_scalar(*dealt(3, 1))
+        second_layer(1)
         second_layer(0)
-        relu(2, 1)
-        for c in range(1, CHUNKS):
-            second_layer(c)
-        for c in range(CHUNKS):
+        relu_vector(*dealt(2, 1))
+        second_layer(2)
+        second_layer(3)
+        for c in (1, 0, 2, 3):
             finish(c)

from contextlib import ExitStack

import concourse.mybir as mybir

K, H, M, T, S = 1024, 512, 128, 1024, 512
FLOPS = 2 * K * H * S + 2 * H * M * S

F32 = mybir.dt.float32
BF16 = mybir.dt.bfloat16
I32 = mybir.dt.int32
U32 = mybir.dt.uint32
U16 = mybir.dt.uint16
U8 = mybir.dt.uint8
FP8X4 = mybir.dt.float8_e4m3fn_x4
FP4X4 = mybir.dt.float4_e2m1fn_x4
MULT = mybir.AluOpType.mult
RELU = mybir.ActivationFunctionType.Relu
IDENTITY = mybir.ActivationFunctionType.Identity

P = 128
PACK = 4
PASSES = K // (P * PACK)
LIST_ROWS = 16
LINE = 4
BLOCK = 32
CHUNK = 128
CHUNKS = S // CHUNK
SCALAR_SHARE = ((52, 92), (44, 44))


def tile_list_hmlp_bias_kernel(tc, xT, w1, w2_words, w2_scales, wgt, b, offs, out):
    nc = tc.nc
    x_planes = xT.rearrange("(a p i) t -> a i p t", p=P, i=PACK)
    w_rows = w1.rearrange("(a p i) r -> a p (i r)", p=P, i=PACK)
    wgt_once = wgt.rearrange("p (h j) -> (p h) j", h=2)[:: LIST_ROWS + 1]

    with ExitStack() as ctx:
        keep = ctx.enter_context(tc.tile_pool(name="keep", bufs=1))
        psum = ctx.enter_context(tc.psum_pool(name="psum", bufs=1))

        def sb(name, cols, dtype, tag=None):
            return keep.tile([P, cols], dtype, name=name, tag=tag or name, align_bytes=64)

        offsets = keep.tile([P, S // LIST_ROWS], U16, name="offsets")
        weights = sb("weights", S, F32)
        wgt_runs = sb("wgt_runs", BLOCK, F32)
        wgt_turned = sb("wgt_turned", BLOCK, F32)
        wgt_repeated = sb("wgt_repeated", S, F32)
        x_raw = [[sb(f"x_raw{a}{i}", T, F32) for i in range(PACK)] for a in range(PASSES)]
        w_raw = [sb(f"w_raw{a}", PACK * H, F32) for a in range(PASSES)]
        picked = [[sb(f"picked{a}{pair}", 2 * S, F32) for pair in range(2)] for a in range(PASSES)]
        weights_third = sb("weights_third", 2 * CHUNK, F32)
        x_bf = [sb(f"x_bf{a}", PACK * S, BF16) for a in range(PASSES)]
        w_bf = [[sb(f"w_bf{a}{half}", PACK * H // 2, BF16) for half in range(2)] for a in range(PASSES)]
        weights_again = sb("weights_again", S, F32)
        x_codes0 = sb("x_codes0", S, U32, tag="weights_again")
        x_early = sb("x_early", S // 2, U32)
        x_late = sb("x_late", S // 2, U32, tag="w_raw1")

        def x_codes(a, j0, j1):
            if a == 0:
                return x_codes0[:, j0:j1]
            return x_early[:, j0:j1] if j1 <= S // 2 else x_late[:, j0 - S // 2 : j1 - S // 2]

        x_scales = [sb(f"x_scales{a}", S, U8) for a in range(PASSES)]
        w_codes = [
            [sb("w_codes00", H // 2, U32)[:], sb("w_codes01", H // 2, U32, tag="weights_third")[:]],
            [sb("w_codes10", H // 2, U32)[:], sb("w_codes11", H // 2, U32)[:]],
        ]
        w_scales = [sb(f"w_scales{a}", H, U8) for a in range(PASSES)]
        h_bf = [sb(f"h_bf{c}", PACK * CHUNK, BF16) for c in range(CHUNKS)]
        h_codes = [sb(f"h_codes{c}", CHUNK, U32) for c in range(CHUNKS)]
        h_scales = [sb(f"h_scales{c}", CHUNK, U8) for c in range(CHUNKS)]
        w2_codes = sb("w2_codes", 2 * M, U8)
        w2_scale_tile = sb("w2_scale_tile", M, U8)
        bias = sb("bias", 1, F32)
        result = [sb(f"result{c}", CHUNK, F32) for c in range(CHUNKS)]
        h_whole = {c: psum.tile([P, PACK * CHUNK], F32, name=f"h_whole{c}") for c in (0, 2, 3)}
        h_halves = [psum.tile([P, 2 * CHUNK], F32, name=f"h_half{half}") for half in range(2)]
        y_acc = {c: psum.tile([P, CHUNK], F32, name=f"y_acc{c}") for c in (0, 2, 3)}
        y_acc[1] = psum.tile([P, CHUNK], F32, name="y_acc1", tag="h_half0")

        def load_x(a, i):
            nc.sync.dma_start(out=x_raw[a][i][:], in_=x_planes[a, i])

        def load_w(a):
            nc.sync.dma_start(out=w_raw[a][:], in_=w_rows[a])

        nc.vector.memset(w2_scale_tile[:].bitcast(U32), 0)

        nc.sync.dma_start(out=wgt_runs[:], in_=wgt_once.rearrange("e (c n) -> e c n", n=BLOCK))
        load_x(0, 0)
        nc.sync.dma_start(offsets[:], offs)
        for plane in range(1, PASSES * PACK - 1):
            load_x(*divmod(plane, PACK))
        load_w(0)
        load_x(1, 3)
        load_w(1)
        nc.sync.dma_start(out=w2_codes[:].bitcast(I32), in_=w2_words[0].bitcast(I32))
        for quadrant in range(4):
            nc.sync.dma_start(
                out=w2_scale_tile[32 * quadrant : 32 * quadrant + 4, :].bitcast(I32),
                in_=w2_scales[0, 4 * quadrant : 4 * quadrant + 4, :].bitcast(I32),
            )
        nc.sync.dma_start(out=bias[:], in_=b.rearrange("(p o) -> p o", o=1))

        def picks(a, pair, j0, j1):
            return picked[a][pair][:].rearrange("p (e j) -> p e j", e=2)[:, :, j0:j1]

        def gather(a, i, j0=0, j1=S, factors=weights):
            nc.vector.tensor_tensor(
                picks(a, i // 2, j0, j1)[:, i % 2],
                x_raw[a][i][:].indirect(offsets[:, j0 // LIST_ROWS : j1 // LIST_ROWS]),
                factors[:, j0:j1],
                MULT,
            )

        def weave_x(copy, a, pair, j0=0, j1=S):
            src = picks(a, pair, j0, j1).rearrange("p e (c n) -> p c e n", n=LINE)
            dst = x_bf[a][:, PACK * j0 : PACK * j1].rearrange("p (c n h e) -> p h c e n", n=LINE, h=2, e=2)[:, pair]
            copy(out=dst, in_=src)

        def weave_dealt(copy, a, pair, c):
            src = picks(a, pair, c * CHUNK, (c + 1) * CHUNK).rearrange("p e (u c n) -> p u c e n", u=2, n=LINE)
            dst = x_bf[a][:, PACK * S // 2 :].rearrange("p (u d c n h e) -> p d h u c e n", u=2, d=2, n=LINE, h=2, e=2)
            copy(out=dst[:, c - 2, pair], in_=src)

        def weave_pair(a, pair):
            weave_x(nc.scalar.copy, a, pair, 0, S // 2)
            for c in (2, 3):
                weave_dealt(nc.scalar.copy, a, pair, c)

        def weave_w_scalar(a, half):
            share = SCALAR_SHARE[a][half]
            src = w_raw[a][:].rearrange("p (i m t) -> p m i t", i=PACK, t=PACK)
            dst = w_bf[a][half][:].rearrange("p (t m i) -> p m i t", t=2, i=PACK)
            nc.scalar.copy(out=dst[:, :share], in_=src[:, :share, :, 2 * half : 2 * half + 2])

        def weave_w_vector(a, half):
            share = SCALAR_SHARE[a][half]
            src = w_raw[a][:].rearrange("p (i m t) -> p m i t", i=PACK, t=PACK)
            dst = w_bf[a][half][:].rearrange("p (t m i) -> p m i t", t=2, i=PACK)
            nc.vector.tensor_copy(out=dst[:, share:], in_=src[:, share:, :, 2 * half : 2 * half + 2])

        def quantize(codes, scales, values):
            nc.vector.quantize_mx(out=codes.bitcast(FP8X4), scales=scales, in_=values)

        def quantize_x(a, j0, j1):
            quantize(x_codes(a, j0, j1), x_scales[a][:, j0:j1], x_bf[a][:, PACK * j0 : PACK * j1])

        def quantize_w(a, t0, t1):
            half, c0, c1 = t0 // 2, t0 % 2 * P, (t1 - t0 // 2 * 2) * P
            quantize(
                w_codes[a][half][:, c0:c1], w_scales[a][:, t0 * P : t1 * P], w_bf[a][half][:, PACK * c0 : PACK * c1]
            )

        def first_layer(a, c, t):
            cols = slice(c * CHUNK, (c + 1) * CHUNK)
            bank, place, last = (h_halves[t // 2], t % 2, 1) if c == 1 else (h_whole[c], t, PACK - 1)
            nc.tensor.matmul_mx(
                out=bank[:, place * CHUNK : (place + 1) * CHUNK],
                lhsT=w_codes[a][t // 2][:, t % 2 * P : (t % 2 + 1) * P].bitcast(FP8X4),
                lhsT_scale=w_scales[a][:, t * P : (t + 1) * P],
                rhs=x_codes(a, cols.start, cols.stop).bitcast(FP8X4),
                rhs_scale=x_scales[a][:, cols],
                start=(a == 0 and place == 0),
                stop=(a == PASSES - 1 and place == last),
            )

        def relu_vector(dst, src):
            nc.vector.tensor_scalar_max(dst, src, 0.0)

        def relu_scalar(dst, src):
            nc.scalar.activation(out=dst, in_=src, func=RELU)

        def by_token(tile, slots=PACK):
            return tile[:].rearrange("p (t n) -> p n t", t=slots)

        def rounded(c):
            return h_bf[c][:].rearrange("p (n t) -> p n t", t=PACK)

        def dealt(bank, half):
            n0 = (bank - 2) * CHUNK // 2
            src = by_token(h_whole[bank])[:, half * CHUNK // 2 : (half + 1) * CHUNK // 2]
            return rounded(2 + half)[:, n0 : n0 + CHUNK // 2], src

        def second_layer(c):
            quantize(h_codes[c][:], h_scales[c][:], h_bf[c][:])
            nc.tensor.matmul_mx(
                out=y_acc[c][:],
                lhsT=w2_codes[:].bitcast(FP4X4),
                lhsT_scale=w2_scale_tile[:],
                rhs=h_codes[c][:].bitcast(FP8X4),
                rhs_scale=h_scales[c][:],
                start=True,
                stop=True,
            )

        def finish(c):
            nc.scalar.activation(out=result[c][:], in_=y_acc[c][:], func=IDENTITY, bias=bias[:, 0:1])
            nc.sync.dma_start(out=out[:, c * CHUNK : (c + 1) * CHUNK], in_=result[c][:])

        nc.vector.transpose(wgt_turned[:], wgt_runs[:])
        repeated = wgt_repeated[:].rearrange("p (c h u) -> p c h u", h=2, u=LIST_ROWS)
        turned = wgt_turned[:].rearrange("p (h c) -> p c h", h=2).unsqueeze(3)
        halves = (slice(0, S // 2), slice(S // 2, S))
        for first in (0, LIST_ROWS // 2):
            runs = slice(first, first + LIST_ROWS // 2)
            nc.vector.tensor_copy(
                out=repeated[:, runs], in_=turned[:, runs].to_broadcast([P, LIST_ROWS // 2, 2, LIST_ROWS])
            )
        for half in halves:
            nc.vector.transpose(weights[:, half], wgt_repeated[:, half])

        for half in halves:
            gather(0, 0, half.start, half.stop)
        gather(0, 1)
        weave_pair(0, 0)
        gather(0, 2)
        gather(0, 3)
        weave_pair(0, 1)
        gather(1, 0)
        nc.scalar.copy(out=weights_again[:, : S - CHUNK], in_=weights[:, : S - CHUNK])
        gather(1, 1, 0, S - CHUNK, weights_again)
        weave_x(nc.scalar.copy, 1, 0, 0, S // 2)
        weave_dealt(nc.scalar.copy, 1, 0, 2)
        gather(1, 1, S - CHUNK, S)
        weave_dealt(nc.scalar.copy, 1, 0, 3)
        gather(1, 2)
        quantize_x(0, 0, S)
        for half in range(2):
            weave_w_scalar(0, half)
            weave_w_vector(0, half)
        quantize_w(0, 0, 2)
        nc.scalar.copy(out=weights_third[:, CHUNK:], in_=weights[:, CHUNK : 2 * CHUNK])
        gather(1, 3, 0, CHUNK)
        gather(1, 3, CHUNK, 2 * CHUNK, weights_third)
        gather(1, 3, 2 * CHUNK, S)
        for c in (0, 1):
            weave_x(nc.scalar.copy, 1, 1, c * CHUNK, (c + 1) * CHUNK)
        weave_dealt(nc.scalar.copy, 1, 1, 3)

        quantize_w(0, 2, 4)
        weave_dealt(nc.vector.tensor_copy, 1, 1, 2)
        for t in range(PACK):
            for c in range(CHUNKS):
                first_layer(0, c, t)
        quantize_x(1, 0, 2 * CHUNK)

        for half in range(2):
            weave_w_scalar(1, half)
            weave_w_vector(1, half)
        for t in range(PACK):
            quantize_w(1, t, t + 1)
        for c in range(CHUNKS // 2, CHUNKS):
            quantize_x(1, c * CHUNK, (c + 1) * CHUNK)
        for t in range(PACK):
            first_layer(1, 1, t)
            first_layer(1, 0, t)
        for c in range(CHUNKS // 2, CHUNKS):
            for t in range(PACK):
                first_layer(1, c, t)
        for half in range(2):
            relu_scalar(rounded(1)[:, :, 2 * half : 2 * half + 2], by_token(h_halves[half], 2))
        relu_vector(rounded(0), by_token(h_whole[0]))
        relu_scalar(*dealt(2, 0))
        relu_scalar(*dealt(3, 0))
        relu_scalar(*dealt(3, 1))
        second_layer(1)
        second_layer(0)
        relu_vector(*dealt(2, 1))
        second_layer(2)
        second_layer(3)
        for c in (1, 0, 2, 3):
            finish(c)
